import numpy as np
import ml_dtypes


def mxq(x, axis, fmt="e4m3"):
    dtype, down = {"e4m3": (ml_dtypes.float8_e4m3fn, 7), "e5m2": (ml_dtypes.float8_e5m2, 14)}[fmt]
    v = np.moveaxis(np.asarray(x, np.float32).astype(ml_dtypes.bfloat16).astype(np.float64), axis, -1)
    blocks = v.reshape(v.shape[:-1] + (-1, 32))
    amax = np.abs(blocks).max(-1, keepdims=True)
    byte = np.maximum(np.where(amax > 0, np.frexp(amax)[1] - 1 + 127, 0) - down, 1)
    scale = np.exp2(byte - 127.0)
    codes = (blocks / scale).astype(np.float32).astype(dtype).astype(np.float64)
    return np.moveaxis((codes * scale).reshape(v.shape), -1, axis)


WIDE = False


def mx_kscale(k):
    if not WIDE:
        return np.ones(k)
    levels = np.array([10, -10, 5, -5, 0])
    if k % 512:
        return np.exp2(np.random.permutation(np.resize(levels, k // 32))).repeat(32)
    a = np.empty((k // 512, 16))
    for p in range(k // 512):
        a[p, :8] = np.random.permutation(np.resize(levels, 8))
        for g in range(8):
            far = levels[np.abs(levels - a[p, g]) >= 10]
            a[p, g + 8] = far[np.random.randint(len(far))]
    return np.exp2(a.ravel()).repeat(32)


BF16 = ml_dtypes.bfloat16


def bf(x):
    return np.asarray(x, np.float32).astype(BF16)


def f64(x):
    return np.asarray(x).astype(np.float64)


E2M1 = np.array([0.0, 0.5, 1.0, 1.5, 2.0, 3.0, 4.0, 6.0, -0.0, -0.5, -1.0, -1.5, -2.0, -3.0, -4.0, -6.0])


def pack_weight(w, fmt):
    k, n = w.shape
    w = f64(bf(w)).reshape(k // 32, 32, n)
    amax = np.abs(w).max(1)
    if fmt == "e4m3":
        byte = np.frexp(amax)[1] - 1 + 127 - 7
    else:
        mant, ex = np.frexp(amax / 6.0)
        byte = np.where(mant > 0.5, ex, ex - 1) + 127
    byte = np.clip(np.where(amax > 0, byte, 1), 1, 254)
    scaled = (w * np.exp2(127.0 - byte)[:, None, :]).reshape(k, n).astype(np.float32)
    by_word = np.ascontiguousarray(scaled.reshape(k // 512, 128, 4, n).transpose(0, 1, 3, 2))
    if fmt == "e4m3":
        words = by_word.astype(ml_dtypes.float8_e4m3fn).view(np.uint8)
    else:
        c = by_word.astype(ml_dtypes.float4_e2m1fn).view(np.uint8) & 0xF
        words = c[..., 0::2] | (c[..., 1::2] << 4)
    return np.ascontiguousarray(words), np.ascontiguousarray(byte.astype(np.uint8).reshape(k // 512, 16, n))


def unpack_weight(words, scales, fmt):
    g, p, n, _ = words.shape
    if fmt == "e4m3":
        vals = np.ascontiguousarray(words).view(ml_dtypes.float8_e4m3fn).astype(np.float64)
    else:
        nib = np.empty((g, p, n, 4), np.uint8)
        nib[..., 0::2] = words & 0xF
        nib[..., 1::2] = words >> 4
        vals = E2M1[nib]
    vals = vals * np.repeat(np.exp2(scales.astype(np.float64) - 127.0), 8, axis=1)[..., None]
    return vals.transpose(0, 1, 3, 2).reshape(g * 512, n)
def pack4(w):
    words, scales = pack_weight(w, "e2m1")
    return words.reshape(words.shape[0], 128, -1), scales


def unpack4(words, scales):
    return unpack_weight(words.reshape(words.shape[0], 128, -1, 2), scales, "e2m1")


M, K1, K2, F, B = 1024, 512, 1536, 1024, 2048


def draw0():
    s1, s2 = mx_kscale(K1), mx_kscale(K2)
    t = mx_kscale(F)
    code_new = np.random.standard_normal((M, K1)) / np.sqrt(K1 + K2)
    code_old = np.random.standard_normal((M, K2)) / np.sqrt(K1 + K2)
    a_new = np.random.standard_normal((K1, F))
    a_old = np.random.standard_normal((K2, F))
    x = np.random.standard_normal((F, B)) / np.sqrt(F)
    old_words, old_scales = pack4(a_old / s2[:, None])
    x_words, x_scales = pack4(x / t[:, None])
    return {"code_new": bf(code_new * s1),
            "data_new": bf(a_new / s1[:, None]),
            "code_old": bf(code_old * s2),
            "old_words": old_words,
            "old_scales": old_scales,
            "mask": bf(0.5 * np.random.standard_normal((M, F))),
            "feature_scale": bf((1 + 0.1 * np.random.standard_normal(F)) * t),
            "x_words": x_words,
            "x_scales": x_scales}


def core(code_new, data_new, code_old, old_words, old_scales, mask, feature_scale, x_words, x_scales):
    new = mxq(f64(code_new), 1, "e4m3") @ mxq(f64(data_new), 0, "e4m3")
    old = mxq(f64(code_old), 1, "e4m3") @ unpack4(old_words, old_scales)
    coded = (new + old + f64(mask)) * f64(feature_scale)
    y = mxq(coded, 1, "e4m3") @ unpack4(x_words, x_scales)
    return y


def e4m3fn_bytes(y):
    return np.clip(np.asarray(y, np.float64), -448.0, 448.0).astype(np.float32).astype(ml_dtypes.float8_e4m3fn).view(np.uint8)


def e4m3fn_values(b):
    return np.asarray(b, np.uint8).view(ml_dtypes.float8_e4m3fn).astype(np.float64)


def setup_inputs():
    d = draw0()
    x0 = np.asarray(d['code_old']).astype(np.float64)
    s = (np.max(np.abs(x0), axis=(0,), keepdims=True) / 448.0).astype(np.float32)
    out = {}
    for k, v in d.items():
        if k == 'code_old':
            out['code_old_bytes'] = e4m3fn_bytes(x0 / s.astype(np.float64))
            out['code_old_scale'] = s
        else:
            out[k] = v
    return out


def reference(code_new, data_new, code_old_bytes, code_old_scale, old_words, old_scales, mask, feature_scale, x_words, x_scales):
    return core(code_new, data_new, e4m3fn_values(code_old_bytes) * code_old_scale.astype(np.float64), old_words, old_scales, mask, feature_scale, x_words, x_scales)

@@ -1,0 +1,330 @@
+from contextlib import ExitStack
+
+import concourse.mybir as mybir
+from concourse.masks import make_identity
+
+M, K1, K2, F, B = 1024, 512, 1536, 1024, 2048
+FLOPS = 2 * M * (K1 + K2) * F + 2 * M * F * B
+
+F32 = mybir.dt.float32
+BF16 = mybir.dt.bfloat16
+I32 = mybir.dt.int32
+U32 = mybir.dt.uint32
+U8 = mybir.dt.uint8
+FP8 = mybir.dt.float8_e4m3fn
+FP8X4 = mybir.dt.float8_e4m3fn_x4
+FP4X4 = mybir.dt.float4_e2m1fn_x4
+ADD = mybir.AluOpType.add
+MULT = mybir.AluOpType.mult
+
+P = 128
+TILES = M // P
+PAIRS = TILES // 2
+NH = 512
+OLD_PASSES = K2 // 512
+PASSES = 1 + OLD_PASSES
+X_PASSES = F // 512
+
+
+def tile_coded_worker_products_s3_kernel(
+    tc, code_new, data_new, code_old_bytes, code_old_scale, old_words, old_scales, mask, feature_scale, x_words, x_scales, out
+):
+    nc = tc.nc
+    with ExitStack() as ctx:
+        keep = ctx.enter_context(tc.tile_pool(name="keep", bufs=1))
+        work = ctx.enter_context(tc.tile_pool(name="work", bufs=3))
+        psum = ctx.enter_context(tc.psum_pool(name="psum", bufs=1))
+        ctx.enter_context(tc.manual_schedule())
+
+        warm = keep.tile([P, 8], F32)
+        nc.vector.memset(warm[:], 0.0)
+        o_sc = keep.tile([P, OLD_PASSES, F], U8, align_bytes=64)
+        x_sc = keep.tile([P, X_PASSES, B], U8, align_bytes=64)
+        nc.vector.memset(o_sc[:].rearrange("p g n -> p (g n)").bitcast(I32), 0)
+        nc.vector.memset(x_sc[:].rearrange("p g n -> p (g n)").bitcast(I32), 0)
+
+        scale_cols = keep.tile([P, K2 // P], F32)
+        nc.scalar.dma_start(out=scale_cols[:], in_=code_old_scale.rearrange("o (p c) -> p (o c)", p=P))
+        fs_cols = keep.tile([P, F // P], BF16)
+        nc.scalar.dma_start(out=fs_cols[:], in_=feature_scale.rearrange("(p c) -> p c", p=P))
+        nc.scalar.copy(out=warm[:, 1:2], in_=warm[:, 0:1])
+        ident = keep.tile([P, P], F32)
+        make_identity(nc, ident[:])
+
+        old_v = code_old_bytes.rearrange("(j p i) k -> j p i k", p=P, i=2)
+        new_v = code_new.rearrange("(j p i) k -> j p i k", p=P, i=2)
+        mask_v = mask.rearrange("(j p i) f -> j p i f", p=P, i=2)
+        out_v = out.rearrange("(j p i) b -> j i p b", p=P, i=2)
+
+        old_tiles = []
+        new_tiles = []
+        mask_tiles = []
+        for j in range(PAIRS):
+            ob = keep.tile([P, 2, K2], U8, name=f"old_bytes_{j}")
+            nw = keep.tile([P, 2, K1], BF16, name=f"new_rows_{j}")
+            mk = keep.tile([P, 2, F], BF16, name=f"mask_rows_{j}")
+            old_tiles.append(ob)
+            new_tiles.append(nw)
+            mask_tiles.append(mk)
+
+        data_raw = []
+        o_words = []
+        for h in range(2):
+            dr = keep.tile([P, 4, NH], BF16, name=f"data_raw_{h}")
+            ow = keep.tile([P, OLD_PASSES, 2 * NH], U8, name=f"old_words_{h}", align_bytes=64)
+            data_raw.append(dr)
+            o_words.append(ow)
+        x_w = []
+        for b in range(B // NH):
+            xw = keep.tile([P, X_PASSES, 2 * NH], U8, name=f"x_words_{b}", align_bytes=64)
+            x_w.append(xw)
+
+        def load_codes(j, i):
+            nc.sync.dma_start(out=old_tiles[j][:, i, :], in_=old_v[j, :, i, :])
+            nc.sync.dma_start(out=new_tiles[j][:, i, :], in_=new_v[j, :, i, :])
+
+        def load_data(h):
+            nc.sync.dma_start(out=data_raw[h][:], in_=data_new.rearrange("(p t) f -> p t f", t=4)[:, :, h * NH : (h + 1) * NH])
+
+        def load_old_words(h):
+            nc.sync.dma_start(out=o_words[h][:], in_=old_words.rearrange("g p n -> p g n")[:, :, 2 * NH * h : 2 * NH * (h + 1)])
+
+        def load_scales(tile, src):
+            for q in range(4):
+                nc.sync.dma_start(
+                    out=tile[32 * q : 32 * q + 4, :, :].bitcast(I32),
+                    in_=src.rearrange("g q n -> q g n")[4 * q : 4 * q + 4, :, :].bitcast(I32),
+                )
+
+        load_codes(0, 0)
+        load_data(0)
+        load_codes(0, 1)
+        load_old_words(0)
+        load_scales(o_sc, old_scales)
+        load_data(1)
+        load_old_words(1)
+        nc.sync.dma_start(out=mask_tiles[0][:], in_=mask_v[0])
+        nc.sync.dma_start(out=old_tiles[1][:], in_=old_v[1])
+        nc.sync.dma_start(out=new_tiles[1][:], in_=new_v[1])
+        load_scales(x_sc, x_scales)
+        for b in range(B // NH):
+            nc.sync.dma_start(out=x_w[b][:], in_=x_words.rearrange("g p n -> p g n")[:, :, 2 * NH * b : 2 * NH * (b + 1)])
+        nc.sync.dma_start(out=mask_tiles[1][:], in_=mask_v[1])
+        for j in range(2, PAIRS):
+            nc.sync.dma_start(out=old_tiles[j][:], in_=old_v[j])
+            nc.sync.dma_start(out=new_tiles[j][:], in_=new_v[j])
+            nc.sync.dma_start(out=mask_tiles[j][:], in_=mask_v[j])
+
+        scale_all = keep.tile([P, K2], F32)
+        fs_all = keep.tile([P, F], F32)
+
+        def spread(bank, cols, c0):
+            for c in range(4):
+                nc.tensor.transpose(bank[:, c, :], cols[:, c0 + c : c0 + c + 1].to_broadcast([P, P]), ident[:])
+
+        def unspread(copy, dst, bank, c0):
+            copy(out=dst[:].rearrange("p (n c) -> p n c", n=P)[:, :, c0 : c0 + 4], in_=bank[:].rearrange("p c n -> p n c"))
+
+        sp0 = psum.tile([P, 4, P], F32, name="sp0", tag="tr", bufs=2)
+        spread(sp0, scale_cols, 0)
+        sp1 = psum.tile([P, 4, P], F32, name="sp1", tag="tr", bufs=2)
+        spread(sp1, scale_cols, 4)
+        sp2 = psum.tile([P, 4, P], F32, name="sp2", tag="trc", bufs=1)
+        spread(sp2, scale_cols, 8)
+        unspread(nc.scalar.copy, scale_all, sp0, 0)
+        unspread(nc.vector.tensor_copy, scale_all, sp1, 4)
+        unspread(nc.scalar.copy, scale_all, sp2, 8)
+
+        prods = {}
+        groups = {}
+        kcodes = {}
+        sums = {}
+        cs = {}
+        cgroups = {}
+        ccodes = {}
+
+        def product(t, g):
+            if g == 0:
+                pr = work.tile([P, K2], BF16, name=f"prod_{t}", tag="prod", bufs=3, align_bytes=64)
+                prods[t] = pr
+            k = slice(512 * g, 512 * (g + 1))
+            nc.vector.tensor_tensor(
+                out=prods[t][:, k], in0=old_tiles[t // 2][:, t % 2, k].bitcast(FP8), in1=scale_all[:, k], op=MULT
+            )
+
+        def code_transposes(t, half):
+            bank = psum.tile([P, 2, 2, P], F32, name=f"tr_{t}_{half}", tag="tr", bufs=2)
+            for s in range(2):
+                g = 2 * half + s
+                words = new_tiles[t // 2][:, t % 2, :].bitcast(F32) if g == 0 else prods[t][:, 512 * (g - 1) : 512 * g].bitcast(F32)
+                for u in range(2):
+                    nc.tensor.transpose(bank[:, s, u, :], words[:, u : 256 : 2], ident[:])
+            if half == 0:
+                gr = work.tile([P, PASSES, P, 4], BF16, name=f"grouped_{t}", tag="grouped", bufs=3, align_bytes=64)
+                groups[t] = gr
+            nc.scalar.copy(
+                out=groups[t][:, 2 * half : 2 * half + 2, :, :].bitcast(F32), in_=bank[:].rearrange("p s u m -> p s m u")
+            )
+
+        def code_quantize(t, half):
+            if half == 0:
+                kc = work.tile([P, PASSES, P], U32, name=f"kcodes_{t}", tag="kcodes", bufs=3, align_bytes=64)
+                ks = work.tile([P, PASSES, P], U8, name=f"kscales_{t}", tag="kscales", bufs=3, align_bytes=64)
+                kcodes[t] = (kc, ks)
+            kc, ks = kcodes[t]
+            s = slice(2 * half, 2 * half + 2)
+            nc.vector.quantize_mx(
+                out=kc[:, s, :].rearrange("p s m -> p (s m)").bitcast(FP8X4),
+                scales=ks[:, s, :].rearrange("p s m -> p (s m)"),
+                in_=groups[t][:, s, :, :].rearrange("p s m t -> p (s m t)"),
+            )
+
+        data_grouped = []
+        data_codes = []
+        data_scales = []
+        for h in range(2):
+            dg = keep.tile([P, NH, 4], BF16, name=f"data_grouped_{h}", align_bytes=64)
+            dc = keep.tile([P, NH], U32, name=f"data_codes_{h}", align_bytes=64)
+            ds = keep.tile([P, NH], U8, name=f"data_scales_{h}", align_bytes=64)
+            data_grouped.append(dg)
+            data_codes.append(dc)
+            data_scales.append(ds)
+
+        def data_interleave(copy, h):
+            copy(out=data_grouped[h][:], in_=data_raw[h][:].rearrange("p t n -> p n t"))
+
+        def data_quantize(h):
+            nc.vector.quantize_mx(
+                out=data_codes[h][:].bitcast(FP8X4),
+                scales=data_scales[h][:],
+                in_=data_grouped[h][:].rearrange("p n t -> p (n t)"),
+            )
+
+        def stage1(t, h):
+            acc = psum.tile([P, NH], F32, name=f"acc1_{t}_{h}", tag=f"acc1_{h}", bufs=1)
+            kc, ks = kcodes[t]
+            for g in range(1, PASSES):
+                nc.tensor.matmul_mx(
+                    out=acc[:],
+                    lhsT=kc[:, g, :].bitcast(FP8X4),
+                    lhsT_scale=ks[:, g, :],
+                    rhs=o_words[h][:, g - 1, :].bitcast(FP4X4),
+                    rhs_scale=o_sc[:, g - 1, NH * h : NH * (h + 1)],
+                    start=(g == 1),
+                    stop=False,
+                )
+            nc.tensor.matmul_mx(
+                out=acc[:],
+                lhsT=kc[:, 0, :].bitcast(FP8X4),
+                lhsT_scale=ks[:, 0, :],
+                rhs=data_codes[h][:].bitcast(FP8X4),
+                rhs_scale=data_scales[h][:],
+                start=False,
+                stop=True,
+            )
+            sums[t, h] = acc
+
+        def add_mask(t, h):
+            s = work.tile([P, NH], F32, name=f"masked_{t}_{h}", tag="masked", bufs=4)
+            nc.vector.tensor_tensor(out=s[:], in0=sums[t, h][:], in1=mask_tiles[t // 2][:, t % 2, NH * h : NH * (h + 1)], op=ADD)
+            cs[t, h] = s
+
+        def scale_features(t, h):
+            c = work.tile([P, 2, P, 2], BF16, name=f"coded_{t}_{h}", tag="coded", bufs=4, align_bytes=64)
+            nc.vector.tensor_tensor(
+                out=c[:],
+                in0=cs[t, h][:].rearrange("p (w u e) -> p u w e", u=2, e=2),
+                in1=fs_all[:, NH * h : NH * (h + 1)].rearrange("p (w u e) -> p u w e", u=2, e=2),
+                op=MULT,
+            )
+            cs[t, h] = c
+
+        def coded_transposes(t):
+            bank = psum.tile([P, 2, 2, P], F32, name=f"trc_{t}", tag="trc", bufs=1)
+            for h in range(2):
+                words = cs[t, h][:].rearrange("p u w e -> p (u w e)").bitcast(F32)
+                for u in range(2):
+                    nc.tensor.transpose(bank[:, h, u, :], words[:, P * u : P * (u + 1)], ident[:])
+            cg = work.tile([P, 2, P, 4], BF16, name=f"coded_grouped_{t}", tag="coded_grouped", bufs=2, align_bytes=64)
+            nc.scalar.copy(out=cg[:].bitcast(F32), in_=bank[:].rearrange("p h u m -> p h m u"))
+            cgroups[t] = cg
+
+        def coded_quantize(t):
+            cc = work.tile([P, 2, P], U32, name=f"ccodes_{t}", tag="ccodes", bufs=2, align_bytes=64)
+            cz = work.tile([P, 2, P], U8, name=f"cscales_{t}", tag="cscales", bufs=2, align_bytes=64)
+            nc.vector.quantize_mx(
+                out=cc[:].rearrange("p h m -> p (h m)").bitcast(FP8X4),
+                scales=cz[:].rearrange("p h m -> p (h m)"),
+                in_=cgroups[t][:].rearrange("p h m t -> p (h m t)"),
+            )
+            ccodes[t] = (cc, cz)
+
+        def stage2(t):
+            cc, cz = ccodes[t]
+            res = work.tile([P, B], F32, name=f"result_{t}", tag="result", bufs=3)
+            for b in range(B // NH):
+                acc = psum.tile([P, NH], F32, name=f"acc2_{t}_{b}", tag="acc2", bufs=3)
+                for g in range(X_PASSES):
+                    nc.tensor.matmul_mx(
+                        out=acc[:],
+                        lhsT=cc[:, g, :].bitcast(FP8X4),
+                        lhsT_scale=cz[:, g, :],
+                        rhs=x_w[b][:, g, :].bitcast(FP4X4),
+                        rhs_scale=x_sc[:, g, NH * b : NH * (b + 1)],
+                        start=(g == 0),
+                        stop=(g == X_PASSES - 1),
+                    )
+                nc.scalar.copy(out=res[:, NH * b : NH * (b + 1)], in_=acc[:])
+                last = t == TILES - 1
+                if last or b % 2 == 1:
+                    cols = slice(NH * b, NH * (b + 1)) if last else slice(NH * (b - 1), NH * (b + 1))
+                    nc.sync.dma_start(out=out_v[t // 2, t % 2, :, cols], in_=res[:, cols])
+
+        for g in range(OLD_PASSES):
+            product(0, g)
+        code_transposes(0, 0)
+        code_transposes(0, 1)
+        fs_f32 = keep.tile([P, F // P], F32)
+        nc.vector.tensor_copy(out=fs_f32[:], in_=fs_cols[:])
+        data_interleave(nc.vector.tensor_copy, 0)
+        data_quantize(0)
+        code_quantize(0, 0)
+        code_quantize(0, 1)
+        fp0 = psum.tile([P, 4, P], F32, name="fp0", tag="acc2", bufs=3)
+        spread(fp0, fs_f32, 0)
+        fp1 = psum.tile([P, 4, P], F32, name="fp1", tag="acc2", bufs=3)
+        spread(fp1, fs_f32, 4)
+        unspread(nc.scalar.copy, fs_all, fp0, 0)
+        unspread(nc.scalar.copy, fs_all, fp1, 4)
+        data_interleave(nc.scalar.copy, 1)
+        for g in range(OLD_PASSES):
+            product(1, g)
+        stage1(0, 0)
+        code_transposes(1, 0)
+        code_transposes(1, 1)
+        data_quantize(1)
+
+        for i in range(TILES):
+            if i + 2 < TILES:
+                product(i + 2, 0)
+                product(i + 2, 1)
+            if i > 0:
+                stage1(i, 0)
+            add_mask(i, 0)
+            if i + 1 < TILES:
+                code_quantize(i + 1, 0)
+                code_quantize(i + 1, 1)
+            stage1(i, 1)
+            add_mask(i, 1)
+            scale_features(i, 0)
+            if i + 2 < TILES:
+                product(i + 2, 2)
+            scale_features(i, 1)
+            if i > 0:
+                stage2(i - 1)
+            coded_transposes(i)
+            if i + 2 < TILES:
+                code_transposes(i + 2, 0)
+                code_transposes(i + 2, 1)
+            coded_quantize(i)
+        stage2(TILES - 1)

@@ -24,6 +24,7 @@ NH = 512
 OLD_PASSES = K2 // 512
 PASSES = 1 + OLD_PASSES
 X_PASSES = F // 512
+STEPPED = 4
 
 
 def tile_coded_worker_products_s3_kernel(
@@ -43,10 +44,10 @@ def tile_coded_worker_products_s3_kernel(
         nc.vector.memset(o_sc[:].rearrange("p g n -> p (g n)").bitcast(I32), 0)
         nc.vector.memset(x_sc[:].rearrange("p g n -> p (g n)").bitcast(I32), 0)
 
-        scale_cols = keep.tile([P, K2 // P], F32)
-        nc.scalar.dma_start(out=scale_cols[:], in_=code_old_scale.rearrange("o (p c) -> p (o c)", p=P))
-        fs_cols = keep.tile([P, F // P], BF16)
-        nc.scalar.dma_start(out=fs_cols[:], in_=feature_scale.rearrange("(p c) -> p c", p=P))
+        scale_cols = keep.tile([P, OLD_PASSES, 4], F32)
+        nc.scalar.dma_start(out=scale_cols[:], in_=code_old_scale.rearrange("o (g p c) -> p (o g) c", p=P, c=4))
+        fs_cols = keep.tile([P, 2, 4], BF16)
+        nc.scalar.dma_start(out=fs_cols[:], in_=feature_scale.rearrange("(g p c) -> p g c", p=P, c=4))
         nc.scalar.copy(out=warm[:, 1:2], in_=warm[:, 0:1])
         ident = keep.tile([P, P], F32)
         make_identity(nc, ident[:])
@@ -96,44 +97,46 @@ def tile_coded_worker_products_s3_kernel(
                     in_=src.rearrange("g q n -> q g n")[4 * q : 4 * q + 4, :, :].bitcast(I32),
                 )
 
-        load_codes(0, 0)
         load_data(0)
+        load_codes(0, 0)
         load_codes(0, 1)
         load_old_words(0)
         load_scales(o_sc, old_scales)
         load_data(1)
         load_old_words(1)
-        nc.sync.dma_start(out=mask_tiles[0][:], in_=mask_v[0])
         nc.sync.dma_start(out=old_tiles[1][:], in_=old_v[1])
         nc.sync.dma_start(out=new_tiles[1][:], in_=new_v[1])
-        load_scales(x_sc, x_scales)
+        nc.sync.dma_start(out=mask_tiles[0][:], in_=mask_v[0])
+        nc.sync.dma_start(out=old_tiles[2][:], in_=old_v[2])
+        nc.sync.dma_start(out=new_tiles[2][:], in_=new_v[2])
         for b in range(B // NH):
             nc.sync.dma_start(out=x_w[b][:], in_=x_words.rearrange("g p n -> p g n")[:, :, 2 * NH * b : 2 * NH * (b + 1)])
+        load_scales(x_sc, x_scales)
         nc.sync.dma_start(out=mask_tiles[1][:], in_=mask_v[1])
-        for j in range(2, PAIRS):
-            nc.sync.dma_start(out=old_tiles[j][:], in_=old_v[j])
-            nc.sync.dma_start(out=new_tiles[j][:], in_=new_v[j])
-            nc.sync.dma_start(out=mask_tiles[j][:], in_=mask_v[j])
+        nc.sync.dma_start(out=old_tiles[3][:], in_=old_v[3])
+        nc.sync.dma_start(out=new_tiles[3][:], in_=new_v[3])
+        nc.sync.dma_start(out=mask_tiles[2][:], in_=mask_v[2])
+        nc.sync.dma_start(out=mask_tiles[3][:], in_=mask_v[3])
 
         scale_all = keep.tile([P, K2], F32)
         fs_all = keep.tile([P, F], F32)
 
-        def spread(bank, cols, c0):
+        def spread(bank, cols):
             for c in range(4):
-                nc.tensor.transpose(bank[:, c, :], cols[:, c0 + c : c0 + c + 1].to_broadcast([P, P]), ident[:])
+                nc.tensor.transpose(bank[:, c, :], cols[:, c : c + 1].to_broadcast([P, P]), ident[:])
 
-        def unspread(copy, dst, bank, c0):
-            copy(out=dst[:].rearrange("p (n c) -> p n c", n=P)[:, :, c0 : c0 + 4], in_=bank[:].rearrange("p c n -> p n c"))
+        def unspread(copy, dst, bank):
+            copy(out=dst.rearrange("p (n c) -> p n c", c=4), in_=bank[:].rearrange("p c n -> p n c"))
 
         sp0 = psum.tile([P, 4, P], F32, name="sp0", tag="tr", bufs=2)
-        spread(sp0, scale_cols, 0)
+        spread(sp0, scale_cols[:, 0, :])
         sp1 = psum.tile([P, 4, P], F32, name="sp1", tag="tr", bufs=2)
-        spread(sp1, scale_cols, 4)
+        spread(sp1, scale_cols[:, 1, :])
         sp2 = psum.tile([P, 4, P], F32, name="sp2", tag="trc", bufs=1)
-        spread(sp2, scale_cols, 8)
-        unspread(nc.scalar.copy, scale_all, sp0, 0)
-        unspread(nc.vector.tensor_copy, scale_all, sp1, 4)
-        unspread(nc.scalar.copy, scale_all, sp2, 8)
+        spread(sp2, scale_cols[:, 2, :])
+        unspread(nc.scalar.copy, scale_all[:, 0:512], sp0)
+        unspread(nc.vector.tensor_copy, scale_all[:, 512:1024], sp1)
+        unspread(nc.scalar.copy, scale_all[:, 1024:1536], sp2)
 
         prods = {}
         groups = {}
@@ -152,13 +155,25 @@ def tile_coded_worker_products_s3_kernel(
                 out=prods[t][:, k], in0=old_tiles[t // 2][:, t % 2, k].bitcast(FP8), in1=scale_all[:, k], op=MULT
             )
 
+        perms = {}
+
+        def permute(t):
+            pm = work.tile([P, PASSES, 2, P], F32, name=f"perm_{t}", tag="perm", bufs=2)
+            nc.scalar.copy(out=pm[:, 0, :, :], in_=new_tiles[t // 2][:, t % 2, :].bitcast(F32).rearrange("p (w u) -> p u w", u=2))
+            nc.scalar.copy(out=pm[:, 1:, :, :], in_=prods[t][:].bitcast(F32).rearrange("p (g w u) -> p g u w", g=OLD_PASSES, u=2))
+            perms[t] = pm
+
         def code_transposes(t, half):
             bank = psum.tile([P, 2, 2, P], F32, name=f"tr_{t}_{half}", tag="tr", bufs=2)
             for s in range(2):
                 g = 2 * half + s
-                words = new_tiles[t // 2][:, t % 2, :].bitcast(F32) if g == 0 else prods[t][:, 512 * (g - 1) : 512 * g].bitcast(F32)
                 for u in range(2):
-                    nc.tensor.transpose(bank[:, s, u, :], words[:, u : 256 : 2], ident[:])
+                    if t < STEPPED:
+                        words = new_tiles[t // 2][:, t % 2, :].bitcast(F32) if g == 0 else prods[t][:, 512 * (g - 1) : 512 * g].bitcast(F32)
+                        words = words[:, u : 256 : 2]
+                    else:
+                        words = perms[t][:, g, u, :]
+                    nc.tensor.transpose(bank[:, s, u, :], words, ident[:])
             if half == 0:
                 gr = work.tile([P, PASSES, P, 4], BF16, name=f"grouped_{t}", tag="grouped", bufs=3, align_bytes=64)
                 groups[t] = gr
@@ -190,8 +205,8 @@ def tile_coded_worker_products_s3_kernel(
             data_codes.append(dc)
             data_scales.append(ds)
 
-        def data_interleave(copy, h):
-            copy(out=data_grouped[h][:], in_=data_raw[h][:].rearrange("p t n -> p n t"))
+        def data_interleave(copy, h, n0, n1):
+            copy(out=data_grouped[h][:, n0:n1, :], in_=data_raw[h][:, :, n0:n1].rearrange("p t n -> p n t"))
 
         def data_quantize(h):
             nc.vector.quantize_mx(
@@ -201,27 +216,21 @@ def tile_coded_worker_products_s3_kernel(
             )
 
         def stage1(t, h):
-            acc = psum.tile([P, NH], F32, name=f"acc1_{t}_{h}", tag=f"acc1_{h}", bufs=1)
+            acc = psum.tile([P, NH], F32, name=f"acc1_{t}_{h}", tag="acc", bufs=5)
             kc, ks = kcodes[t]
-            for g in range(1, PASSES):
+            order = [1, 2, 3, 0] if h == 1 else [1, 0, 2, 3]
+            for n, g in enumerate(order):
+                rhs = data_codes[h][:].bitcast(FP8X4) if g == 0 else o_words[h][:, g - 1, :].bitcast(FP4X4)
+                rhs_scale = data_scales[h][:] if g == 0 else o_sc[:, g - 1, NH * h : NH * (h + 1)]
                 nc.tensor.matmul_mx(
                     out=acc[:],
                     lhsT=kc[:, g, :].bitcast(FP8X4),
                     lhsT_scale=ks[:, g, :],
-                    rhs=o_words[h][:, g - 1, :].bitcast(FP4X4),
-                    rhs_scale=o_sc[:, g - 1, NH * h : NH * (h + 1)],
-                    start=(g == 1),
-                    stop=False,
+                    rhs=rhs,
+                    rhs_scale=rhs_scale,
+                    start=(n == 0),
+                    stop=(n == PASSES - 1),
                 )
-            nc.tensor.matmul_mx(
-                out=acc[:],
-                lhsT=kc[:, 0, :].bitcast(FP8X4),
-                lhsT_scale=ks[:, 0, :],
-                rhs=data_codes[h][:].bitcast(FP8X4),
-                rhs_scale=data_scales[h][:],
-                start=False,
-                stop=True,
-            )
             sums[t, h] = acc
 
         def add_mask(t, h):
@@ -263,7 +272,7 @@ def tile_coded_worker_products_s3_kernel(
             cc, cz = ccodes[t]
             res = work.tile([P, B], F32, name=f"result_{t}", tag="result", bufs=3)
             for b in range(B // NH):
-                acc = psum.tile([P, NH], F32, name=f"acc2_{t}_{b}", tag="acc2", bufs=3)
+                acc = psum.tile([P, NH], F32, name=f"acc2_{t}_{b}", tag="acc", bufs=5)
                 for g in range(X_PASSES):
                     nc.tensor.matmul_mx(
                         out=acc[:],
@@ -280,51 +289,95 @@ def tile_coded_worker_products_s3_kernel(
                     cols = slice(NH * b, NH * (b + 1)) if last else slice(NH * (b - 1), NH * (b + 1))
                     nc.sync.dma_start(out=out_v[t // 2, t % 2, :, cols], in_=res[:, cols])
 
+        data_interleave(nc.vector.tensor_copy, 0, 0, NH)
         for g in range(OLD_PASSES):
             product(0, g)
         code_transposes(0, 0)
         code_transposes(0, 1)
-        fs_f32 = keep.tile([P, F // P], F32)
-        nc.vector.tensor_copy(out=fs_f32[:], in_=fs_cols[:])
-        data_interleave(nc.vector.tensor_copy, 0)
         data_quantize(0)
+        fs_f32 = keep.tile([P, 2, 4], F32)
+        nc.vector.tensor_copy(out=fs_f32[:], in_=fs_cols[:])
+        product(1, 0)
         code_quantize(0, 0)
+        product(1, 1)
         code_quantize(0, 1)
-        fp0 = psum.tile([P, 4, P], F32, name="fp0", tag="acc2", bufs=3)
-        spread(fp0, fs_f32, 0)
-        fp1 = psum.tile([P, 4, P], F32, name="fp1", tag="acc2", bufs=3)
-        spread(fp1, fs_f32, 4)
-        unspread(nc.scalar.copy, fs_all, fp0, 0)
-        unspread(nc.scalar.copy, fs_all, fp1, 4)
-        data_interleave(nc.scalar.copy, 1)
-        for g in range(OLD_PASSES):
-            product(1, g)
+        product(1, 2)
+        data_interleave(nc.scalar.copy, 1, 0, 256)
+        data_interleave(nc.vector.tensor_copy, 1, 256, 512)
         stage1(0, 0)
         code_transposes(1, 0)
         code_transposes(1, 1)
         data_quantize(1)
+        stage1(0, 1)
+        fp0 = psum.tile([P, 4, P], F32, name="fp0", tag="tr", bufs=2)
+        spread(fp0, fs_f32[:, 0, :])
+        fp1 = psum.tile([P, 4, P], F32, name="fp1", tag="tr", bufs=2)
+        spread(fp1, fs_f32[:, 1, :])
+        unspread(nc.scalar.copy, fs_all[:, 0:512], fp0)
+        unspread(nc.scalar.copy, fs_all[:, 512:1024], fp1)
+        product(2, 0)
+        code_quantize(1, 0)
+        product(2, 1)
+        code_quantize(1, 1)
+        product(2, 2)
+        add_mask(0, 0)
+        add_mask(0, 1)
+        stage1(1, 0)
+        code_transposes(2, 0)
+        code_transposes(2, 1)
+        stage1(1, 1)
+        scale_features(0, 0)
+        scale_features(0, 1)
+        code_quantize(2, 0)
+        code_quantize(2, 1)
+        for g in range(OLD_PASSES):
+            product(3, g)
+        coded_transposes(0)
+        stage1(2, 0)
+        stage1(2, 1)
+        coded_quantize(0)
+        code_transposes(3, 0)
+        code_transposes(3, 1)
+        add_mask(1, 0)
+        add_mask(1, 1)
+        scale_features(1, 0)
+        scale_features(1, 1)
+        code_quantize(3, 0)
+        code_quantize(3, 1)
+        add_mask(2, 0)
+        add_mask(2, 1)
+        stage2(0)
+        for g in range(OLD_PASSES):
+            product(4, g)
+        scale_features(2, 0)
+        scale_features(2, 1)
+        coded_transposes(1)
+        coded_quantize(1)
 
-        for i in range(TILES):
+        for i in range(3, TILES):
+            if i + 1 < TILES:
+                permute(i + 1)
+            stage1(i, 0)
             if i + 2 < TILES:
                 product(i + 2, 0)
                 product(i + 2, 1)
-            if i > 0:
-                stage1(i, 0)
             add_mask(i, 0)
+            if i + 2 < TILES:
+                product(i + 2, 2)
+            stage1(i, 1)
+            add_mask(i, 1)
+            coded_transposes(i - 1)
+            if i + 1 < TILES:
+                code_transposes(i + 1, 0)
+                code_transposes(i + 1, 1)
+            scale_features(i, 0)
+            coded_quantize(i - 1)
             if i + 1 < TILES:
                 code_quantize(i + 1, 0)
                 code_quantize(i + 1, 1)
-            stage1(i, 1)
-            add_mask(i, 1)
-            scale_features(i, 0)
-            if i + 2 < TILES:
-                product(i + 2, 2)
             scale_features(i, 1)
-            if i > 0:
-                stage2(i - 1)
-            coded_transposes(i)
-            if i + 2 < TILES:
-                code_transposes(i + 2, 0)
-                code_transposes(i + 2, 1)
-            coded_quantize(i)
+            stage2(i - 2)
+        coded_transposes(TILES - 1)
+        stage2(TILES - 2)
+        coded_quantize(TILES - 1)
         stage2(TILES - 1)

@@ -16,6 +16,7 @@ FP8X4 = mybir.dt.float8_e4m3fn_x4
 FP4X4 = mybir.dt.float4_e2m1fn_x4
 ADD = mybir.AluOpType.add
 MULT = mybir.AluOpType.mult
+COPY = mybir.ActivationFunctionType.Copy
 
 P = 128
 TILES = M // P
@@ -24,7 +25,6 @@ NH = 512
 OLD_PASSES = K2 // 512
 PASSES = 1 + OLD_PASSES
 X_PASSES = F // 512
-STEPPED = 4
 
 
 def tile_coded_worker_products_s3_kernel(
@@ -44,8 +44,12 @@ def tile_coded_worker_products_s3_kernel(
         nc.vector.memset(o_sc[:].rearrange("p g n -> p (g n)").bitcast(I32), 0)
         nc.vector.memset(x_sc[:].rearrange("p g n -> p (g n)").bitcast(I32), 0)
 
-        scale_cols = keep.tile([P, OLD_PASSES, 4], F32)
-        nc.scalar.dma_start(out=scale_cols[:], in_=code_old_scale.rearrange("o (g p c) -> p (o g) c", p=P, c=4))
+        scale_cols = []
+        for g in range(OLD_PASSES):
+            sc = keep.tile([P, 4], F32, name=f"scale_cols_{g}")
+            nc.scalar.dma_start(out=sc[:], in_=code_old_scale.rearrange("o (g p c) -> g p (o c)", p=P, c=4)[g])
+            scale_cols.append(sc)
+        fs_f32 = keep.tile([P, 2, 4], F32)
         fs_cols = keep.tile([P, 2, 4], BF16)
         nc.scalar.dma_start(out=fs_cols[:], in_=feature_scale.rearrange("(g p c) -> p g c", p=P, c=4))
         nc.scalar.copy(out=warm[:, 1:2], in_=warm[:, 0:1])
@@ -76,13 +80,9 @@ def tile_coded_worker_products_s3_kernel(
             data_raw.append(dr)
             o_words.append(ow)
         x_w = []
-        for b in range(B // NH):
-            xw = keep.tile([P, X_PASSES, 2 * NH], U8, name=f"x_words_{b}", align_bytes=64)
+        for g in range(X_PASSES):
+            xw = keep.tile([P, 2 * B], U8, name=f"x_words_{g}", align_bytes=64)
             x_w.append(xw)
-
-        def load_codes(j, i):
-            nc.sync.dma_start(out=old_tiles[j][:, i, :], in_=old_v[j, :, i, :])
-            nc.sync.dma_start(out=new_tiles[j][:, i, :], in_=new_v[j, :, i, :])
 
         def load_data(h):
             nc.sync.dma_start(out=data_raw[h][:], in_=data_new.rearrange("(p t) f -> p t f", t=4)[:, :, h * NH : (h + 1) * NH])
@@ -97,29 +97,49 @@ def tile_coded_worker_products_s3_kernel(
                     in_=src.rearrange("g q n -> q g n")[4 * q : 4 * q + 4, :, :].bitcast(I32),
                 )
 
-        load_data(0)
-        load_codes(0, 0)
-        load_codes(0, 1)
-        load_old_words(0)
-        load_scales(o_sc, old_scales)
-        load_data(1)
-        load_old_words(1)
-        nc.sync.dma_start(out=old_tiles[1][:], in_=old_v[1])
-        nc.sync.dma_start(out=new_tiles[1][:], in_=new_v[1])
-        nc.sync.dma_start(out=mask_tiles[0][:], in_=mask_v[0])
-        nc.sync.dma_start(out=old_tiles[2][:], in_=old_v[2])
-        nc.sync.dma_start(out=new_tiles[2][:], in_=new_v[2])
-        for b in range(B // NH):
-            nc.sync.dma_start(out=x_w[b][:], in_=x_words.rearrange("g p n -> p g n")[:, :, 2 * NH * b : 2 * NH * (b + 1)])
-        load_scales(x_sc, x_scales)
-        nc.sync.dma_start(out=mask_tiles[1][:], in_=mask_v[1])
-        nc.sync.dma_start(out=old_tiles[3][:], in_=old_v[3])
-        nc.sync.dma_start(out=new_tiles[3][:], in_=new_v[3])
-        nc.sync.dma_start(out=mask_tiles[2][:], in_=mask_v[2])
-        nc.sync.dma_start(out=mask_tiles[3][:], in_=mask_v[3])
+        def load_x(g):
+            nc.sync.dma_start(out=x_w[g][:], in_=x_words[g])
 
+        def load_old_pair(j):
+            nc.sync.dma_start(out=old_tiles[j][:], in_=old_v[j])
+
+        def load_new_pair(j):
+            nc.sync.dma_start(out=new_tiles[j][:], in_=new_v[j])
+
+        def load_mask(j):
+            nc.sync.dma_start(out=mask_tiles[j][:], in_=mask_v[j])
+
+        def load_codes(i):
+            nc.sync.dma_start(out=old_tiles[0][:, i, :], in_=old_v[0, :, i, :])
+            nc.sync.dma_start(out=new_tiles[0][:, i, :], in_=new_v[0, :, i, :])
+
+        load_codes(0)
+        load_data(0)
+        load_data(1)
+        load_codes(1)
+        load_old_pair(1)
+        load_scales(o_sc, old_scales)
+        load_old_words(0)
+        load_old_words(1)
+        load_new_pair(1)
+        load_mask(0)
+        load_mask(1)
+        load_old_pair(2)
+        load_x(1)
+        load_new_pair(2)
+        load_x(0)
+        load_scales(x_sc, x_scales)
+        load_mask(2)
+        load_old_pair(3)
+        load_mask(3)
+        load_new_pair(3)
         scale_all = keep.tile([P, K2], F32)
         fs_all = keep.tile([P, F], F32)
+
+        def spread_features(h):
+            bank = psum.tile([P, 4, P], F32, name=f"fs_{h}", tag="tr", bufs=2)
+            spread(bank, fs_f32[:, h, :])
+            unspread(nc.scalar.copy, fs_all[:, NH * h : NH * (h + 1)], bank)
 
         def spread(bank, cols):
             for c in range(4):
@@ -129,14 +149,15 @@ def tile_coded_worker_products_s3_kernel(
             copy(out=dst.rearrange("p (n c) -> p n c", c=4), in_=bank[:].rearrange("p c n -> p n c"))
 
         sp0 = psum.tile([P, 4, P], F32, name="sp0", tag="tr", bufs=2)
-        spread(sp0, scale_cols[:, 0, :])
+        spread(sp0, scale_cols[0])
         sp1 = psum.tile([P, 4, P], F32, name="sp1", tag="tr", bufs=2)
-        spread(sp1, scale_cols[:, 1, :])
+        spread(sp1, scale_cols[1])
         sp2 = psum.tile([P, 4, P], F32, name="sp2", tag="trc", bufs=1)
-        spread(sp2, scale_cols[:, 2, :])
+        spread(sp2, scale_cols[2])
         unspread(nc.scalar.copy, scale_all[:, 0:512], sp0)
-        unspread(nc.vector.tensor_copy, scale_all[:, 512:1024], sp1)
+        unspread(nc.scalar.copy, scale_all[:, 512:1024], sp1)
         unspread(nc.scalar.copy, scale_all[:, 1024:1536], sp2)
+        nc.scalar.copy(out=fs_f32[:], in_=fs_cols[:])
 
         prods = {}
         groups = {}
@@ -146,11 +167,11 @@ def tile_coded_worker_products_s3_kernel(
         cgroups = {}
         ccodes = {}
 
-        def product(t, g):
-            if g == 0:
+        def product(t, g0=0, g1=OLD_PASSES):
+            if g0 == 0:
                 pr = work.tile([P, K2], BF16, name=f"prod_{t}", tag="prod", bufs=3, align_bytes=64)
                 prods[t] = pr
-            k = slice(512 * g, 512 * (g + 1))
+            k = slice(512 * g0, 512 * g1)
             nc.vector.tensor_tensor(
                 out=prods[t][:, k], in0=old_tiles[t // 2][:, t % 2, k].bitcast(FP8), in1=scale_all[:, k], op=MULT
             )
@@ -163,12 +184,17 @@ def tile_coded_worker_products_s3_kernel(
             nc.scalar.copy(out=pm[:, 1:, :, :], in_=prods[t][:].bitcast(F32).rearrange("p (g w u) -> p g u w", g=OLD_PASSES, u=2))
             perms[t] = pm
 
+        def warm_up(n):
+            bank = psum.tile([P, NH], F32, name="warm_bank", tag="acc", bufs=5)
+            for k in range(n):
+                nc.tensor.matmul(bank[:], lhsT=new_tiles[0][:, 0, 0:P], rhs=new_tiles[0][:, 0, :], start=True, stop=True)
+
         def code_transposes(t, half):
             bank = psum.tile([P, 2, 2, P], F32, name=f"tr_{t}_{half}", tag="tr", bufs=2)
             for s in range(2):
                 g = 2 * half + s
                 for u in range(2):
-                    if t < STEPPED:
+                    if t not in perms:
                         words = new_tiles[t // 2][:, t % 2, :].bitcast(F32) if g == 0 else prods[t][:, 512 * (g - 1) : 512 * g].bitcast(F32)
                         words = words[:, u : 256 : 2]
                     else:
@@ -181,13 +207,13 @@ def tile_coded_worker_products_s3_kernel(
                 out=groups[t][:, 2 * half : 2 * half + 2, :, :].bitcast(F32), in_=bank[:].rearrange("p s u m -> p s m u")
             )
 
-        def code_quantize(t, half):
-            if half == 0:
+        def code_quantize(t, g0=0, g1=PASSES):
+            if g0 == 0:
                 kc = work.tile([P, PASSES, P], U32, name=f"kcodes_{t}", tag="kcodes", bufs=3, align_bytes=64)
                 ks = work.tile([P, PASSES, P], U8, name=f"kscales_{t}", tag="kscales", bufs=3, align_bytes=64)
                 kcodes[t] = (kc, ks)
             kc, ks = kcodes[t]
-            s = slice(2 * half, 2 * half + 2)
+            s = slice(g0, g1)
             nc.vector.quantize_mx(
                 out=kc[:, s, :].rearrange("p s m -> p (s m)").bitcast(FP8X4),
                 scales=ks[:, s, :].rearrange("p s m -> p (s m)"),
@@ -234,26 +260,38 @@ def tile_coded_worker_products_s3_kernel(
             sums[t, h] = acc
 
         def add_mask(t, h):
-            s = work.tile([P, NH], F32, name=f"masked_{t}_{h}", tag="masked", bufs=4)
-            nc.vector.tensor_tensor(out=s[:], in0=sums[t, h][:], in1=mask_tiles[t // 2][:, t % 2, NH * h : NH * (h + 1)], op=ADD)
-            cs[t, h] = s
+            if h == 0:
+                s = work.tile([P, F], F32, name=f"masked_{t}", tag="masked", bufs=2)
+                cs[t] = s
+            cols = slice(NH * h, NH * (h + 1))
+            nc.vector.tensor_tensor(out=cs[t][:, cols], in0=sums[t, h][:], in1=mask_tiles[t // 2][:, t % 2, cols], op=ADD)
 
-        def scale_features(t, h):
-            c = work.tile([P, 2, P, 2], BF16, name=f"coded_{t}_{h}", tag="coded", bufs=4, align_bytes=64)
+        def scale_features(t):
+            c = work.tile([P, 2, 2 * P, 2], BF16, name=f"coded_{t}", tag="coded", bufs=2, align_bytes=64)
             nc.vector.tensor_tensor(
                 out=c[:],
-                in0=cs[t, h][:].rearrange("p (w u e) -> p u w e", u=2, e=2),
-                in1=fs_all[:, NH * h : NH * (h + 1)].rearrange("p (w u e) -> p u w e", u=2, e=2),
+                in0=cs[t][:].rearrange("p (w u e) -> p u w e", u=2, e=2),
+                in1=fs_all[:].rearrange("p (w u e) -> p u w e", u=2, e=2),
                 op=MULT,
             )
-            cs[t, h] = c
+            cs[t] = c
+
+        def coded_early(t, h):
+            bank = psum.tile([P, 4, P], F32, name=f"tre_{t}_{h}", tag="trc", bufs=1)
+            if h == 0:
+                cg = work.tile([P, 2, P, 4], BF16, name=f"coded_grouped_{t}", tag="coded_grouped", bufs=2, align_bytes=64)
+                cgroups[t] = cg
+            for c in range(4):
+                nc.tensor.transpose(bank[:, c, :], cs[t][:, NH * h + c : NH * (h + 1) : 4], ident[:])
+            for c in range(4):
+                nc.scalar.activation(out=cgroups[t][:, h, :, c], in_=bank[:, c, :], func=COPY, scale=fs_f32[:, h, c : c + 1])
 
         def coded_transposes(t):
             bank = psum.tile([P, 2, 2, P], F32, name=f"trc_{t}", tag="trc", bufs=1)
+            words = cs[t][:].rearrange("p u w e -> p (u w e)").bitcast(F32)
             for h in range(2):
-                words = cs[t, h][:].rearrange("p u w e -> p (u w e)").bitcast(F32)
                 for u in range(2):
-                    nc.tensor.transpose(bank[:, h, u, :], words[:, P * u : P * (u + 1)], ident[:])
+                    nc.tensor.transpose(bank[:, h, u, :], words[:, 2 * P * u + P * h : 2 * P * u + P * (h + 1)], ident[:])
             cg = work.tile([P, 2, P, 4], BF16, name=f"coded_grouped_{t}", tag="coded_grouped", bufs=2, align_bytes=64)
             nc.scalar.copy(out=cg[:].bitcast(F32), in_=bank[:].rearrange("p h u m -> p h m u"))
             cgroups[t] = cg
@@ -278,106 +316,96 @@ def tile_coded_worker_products_s3_kernel(
                         out=acc[:],
                         lhsT=cc[:, g, :].bitcast(FP8X4),
                         lhsT_scale=cz[:, g, :],
-                        rhs=x_w[b][:, g, :].bitcast(FP4X4),
+                        rhs=x_w[g][:, 2 * NH * b : 2 * NH * (b + 1)].bitcast(FP4X4),
                         rhs_scale=x_sc[:, g, NH * b : NH * (b + 1)],
                         start=(g == 0),
                         stop=(g == X_PASSES - 1),
                     )
-                nc.scalar.copy(out=res[:, NH * b : NH * (b + 1)], in_=acc[:])
                 last = t == TILES - 1
+                if last and b == B // NH - 1:
+                    nc.scalar.copy(out=res[:, NH * b : NH * b + NH // 2], in_=acc[:, : NH // 2])
+                    nc.vector.tensor_copy(out=res[:, NH * b + NH // 2 : NH * (b + 1)], in_=acc[:, NH // 2 :])
+                elif t >= TILES - 2 and b % 2 == 0:
+                    nc.vector.tensor_copy(out=res[:, NH * b : NH * (b + 1)], in_=acc[:])
+                else:
+                    nc.scalar.copy(out=res[:, NH * b : NH * (b + 1)], in_=acc[:])
                 if last or b % 2 == 1:
                     cols = slice(NH * b, NH * (b + 1)) if last else slice(NH * (b - 1), NH * (b + 1))
                     nc.sync.dma_start(out=out_v[t // 2, t % 2, :, cols], in_=res[:, cols])
 
-        data_interleave(nc.vector.tensor_copy, 0, 0, NH)
-        for g in range(OLD_PASSES):
-            product(0, g)
+        product(0, 0, 1)
+        data_interleave(nc.scalar.copy, 0, 0, 256)
+        spread_features(0)
+        product(0, 1, 2)
+        product(0, 2, 3)
+        data_interleave(nc.vector.tensor_copy, 0, 256, 512)
+        data_interleave(nc.scalar.copy, 1, 0, 384)
+        data_interleave(nc.vector.tensor_copy, 1, 384, 512)
         code_transposes(0, 0)
-        code_transposes(0, 1)
         data_quantize(0)
-        fs_f32 = keep.tile([P, 2, 4], F32)
-        nc.vector.tensor_copy(out=fs_f32[:], in_=fs_cols[:])
-        product(1, 0)
-        code_quantize(0, 0)
-        product(1, 1)
-        code_quantize(0, 1)
-        product(1, 2)
-        data_interleave(nc.scalar.copy, 1, 0, 256)
-        data_interleave(nc.vector.tensor_copy, 1, 256, 512)
-        stage1(0, 0)
-        code_transposes(1, 0)
-        code_transposes(1, 1)
+        product(1)
+        code_transposes(0, 1)
         data_quantize(1)
+        code_quantize(0, 0, 2)
+        warm_up(6)
+        code_transposes(1, 0)
+        code_quantize(0, 2, 4)
+        code_transposes(1, 1)
+        product(2)
+        stage1(0, 0)
+        code_quantize(1)
+        spread_features(1)
         stage1(0, 1)
-        fp0 = psum.tile([P, 4, P], F32, name="fp0", tag="tr", bufs=2)
-        spread(fp0, fs_f32[:, 0, :])
-        fp1 = psum.tile([P, 4, P], F32, name="fp1", tag="tr", bufs=2)
-        spread(fp1, fs_f32[:, 1, :])
-        unspread(nc.scalar.copy, fs_all[:, 0:512], fp0)
-        unspread(nc.scalar.copy, fs_all[:, 512:1024], fp1)
-        product(2, 0)
-        code_quantize(1, 0)
-        product(2, 1)
-        code_quantize(1, 1)
-        product(2, 2)
+        permute(2)
+        product(3)
+        stage1(1, 1)
         add_mask(0, 0)
-        add_mask(0, 1)
-        stage1(1, 0)
+        permute(3)
         code_transposes(2, 0)
         code_transposes(2, 1)
-        stage1(1, 1)
-        scale_features(0, 0)
-        scale_features(0, 1)
-        code_quantize(2, 0)
-        code_quantize(2, 1)
-        for g in range(OLD_PASSES):
-            product(3, g)
-        coded_transposes(0)
-        stage1(2, 0)
-        stage1(2, 1)
-        coded_quantize(0)
+        stage1(1, 0)
+        add_mask(0, 1)
+        scale_features(0)
         code_transposes(3, 0)
+        coded_transposes(0)
         code_transposes(3, 1)
+        code_quantize(2)
+        stage1(2, 0)
         add_mask(1, 0)
+        stage1(2, 1)
         add_mask(1, 1)
-        scale_features(1, 0)
-        scale_features(1, 1)
-        code_quantize(3, 0)
-        code_quantize(3, 1)
+        coded_quantize(0)
+        scale_features(1)
         add_mask(2, 0)
         add_mask(2, 1)
+        code_quantize(3)
         stage2(0)
-        for g in range(OLD_PASSES):
-            product(4, g)
-        scale_features(2, 0)
-        scale_features(2, 1)
+        product(4)
         coded_transposes(1)
+        scale_features(2)
         coded_quantize(1)
 
         for i in range(3, TILES):
             if i + 1 < TILES:
                 permute(i + 1)
             stage1(i, 0)
-            if i + 2 < TILES:
-                product(i + 2, 0)
-                product(i + 2, 1)
-            add_mask(i, 0)
-            if i + 2 < TILES:
-                product(i + 2, 2)
             stage1(i, 1)
+            if i + 2 < TILES:
+                product(i + 2)
+            add_mask(i, 0)
             add_mask(i, 1)
             coded_transposes(i - 1)
             if i + 1 < TILES:
                 code_transposes(i + 1, 0)
                 code_transposes(i + 1, 1)
-            scale_features(i, 0)
-            coded_quantize(i - 1)
-            if i + 1 < TILES:
-                code_quantize(i + 1, 0)
-                code_quantize(i + 1, 1)
-            scale_features(i, 1)
+                coded_quantize(i - 1)
+                code_quantize(i + 1)
+                scale_features(i)
+            else:
+                scale_features(i)
+                coded_quantize(i - 1)
             stage2(i - 2)
         coded_transposes(TILES - 1)
-        stage2(TILES - 2)
         coded_quantize(TILES - 1)
+        stage2(TILES - 2)
         stage2(TILES - 1)

@@ -72,20 +72,18 @@ def tile_coded_worker_products_s3_kernel(
             new_tiles.append(nw)
             mask_tiles.append(mk)
 
-        data_raw = []
+        data_raw = keep.tile([P, 4, F], BF16)
         o_words = []
         for h in range(2):
-            dr = keep.tile([P, 4, NH], BF16, name=f"data_raw_{h}")
             ow = keep.tile([P, OLD_PASSES, 2 * NH], U8, name=f"old_words_{h}", align_bytes=64)
-            data_raw.append(dr)
             o_words.append(ow)
         x_w = []
         for g in range(X_PASSES):
             xw = keep.tile([P, 2 * B], U8, name=f"x_words_{g}", align_bytes=64)
             x_w.append(xw)
 
-        def load_data(h):
-            nc.sync.dma_start(out=data_raw[h][:], in_=data_new.rearrange("(p t) f -> p t f", t=4)[:, :, h * NH : (h + 1) * NH])
+        def load_data():
+            nc.sync.dma_start(out=data_raw[:], in_=data_new.rearrange("(p t) f -> p t f", t=4))
 
         def load_old_words(h):
             nc.sync.dma_start(out=o_words[h][:], in_=old_words.rearrange("g p n -> p g n")[:, :, 2 * NH * h : 2 * NH * (h + 1)])
@@ -114,25 +112,24 @@ def tile_coded_worker_products_s3_kernel(
             nc.sync.dma_start(out=new_tiles[0][:, i, :], in_=new_v[0, :, i, :])
 
         load_codes(0)
-        load_data(0)
-        load_data(1)
+        load_data()
         load_codes(1)
         load_old_pair(1)
-        load_scales(o_sc, old_scales)
         load_old_words(0)
+        load_scales(o_sc, old_scales)
         load_old_words(1)
         load_new_pair(1)
         load_mask(0)
         load_mask(1)
-        load_old_pair(2)
-        load_x(1)
         load_new_pair(2)
         load_x(0)
         load_scales(x_sc, x_scales)
-        load_mask(2)
-        load_old_pair(3)
-        load_mask(3)
+        load_x(1)
+        load_old_pair(2)
         load_new_pair(3)
+        load_mask(2)
+        load_mask(3)
+        load_old_pair(3)
         scale_all = keep.tile([P, K2], F32)
         fs_all = keep.tile([P, F], F32)
 
@@ -232,7 +229,7 @@ def tile_coded_worker_products_s3_kernel(
             data_scales.append(ds)
 
         def data_interleave(copy, h, n0, n1):
-            copy(out=data_grouped[h][:, n0:n1, :], in_=data_raw[h][:, :, n0:n1].rearrange("p t n -> p n t"))
+            copy(out=data_grouped[h][:, n0:n1, :], in_=data_raw[:, :, NH * h + n0 : NH * h + n1].rearrange("p t n -> p n t"))
 
         def data_quantize(h):
             nc.vector.quantize_mx(
@@ -258,6 +255,11 @@ def tile_coded_worker_products_s3_kernel(
                     stop=(n == PASSES - 1),
                 )
             sums[t, h] = acc
+
+        def evacuate(t, h):
+            ev = work.tile([P, NH], F32, name=f"evac_{t}_{h}", tag="evac", bufs=6)
+            nc.scalar.copy(out=ev[:], in_=sums[t, h][:])
+            sums[t, h] = ev
 
         def add_mask(t, h):
             if h == 0:
@@ -334,54 +336,56 @@ def tile_coded_worker_products_s3_kernel(
                     nc.sync.dma_start(out=out_v[t // 2, t % 2, :, cols], in_=res[:, cols])
 
         product(0, 0, 1)
-        data_interleave(nc.scalar.copy, 0, 0, 256)
+        code_transposes(0, 0)
         spread_features(0)
         product(0, 1, 2)
         product(0, 2, 3)
-        data_interleave(nc.vector.tensor_copy, 0, 256, 512)
-        data_interleave(nc.scalar.copy, 1, 0, 384)
-        data_interleave(nc.vector.tensor_copy, 1, 384, 512)
-        code_transposes(0, 0)
-        data_quantize(0)
-        product(1)
+        data_interleave(nc.vector.tensor_copy, 0, 128, 512)
+        data_interleave(nc.scalar.copy, 0, 0, 128)
         code_transposes(0, 1)
-        data_quantize(1)
+        product(1)
+        data_quantize(0)
+        spread_features(1)
         code_quantize(0, 0, 2)
+        data_interleave(nc.scalar.copy, 1, 0, 384)
+        code_quantize(0, 2, 4)
         warm_up(6)
         code_transposes(1, 0)
-        code_quantize(0, 2, 4)
-        code_transposes(1, 1)
+        data_interleave(nc.vector.tensor_copy, 1, 384, 512)
         product(2)
+        code_transposes(1, 1)
         stage1(0, 0)
+        data_quantize(1)
         code_quantize(1)
-        spread_features(1)
-        stage1(0, 1)
-        permute(2)
         product(3)
-        stage1(1, 1)
-        add_mask(0, 0)
+        stage1(0, 1)
+        evacuate(0, 0)
         permute(3)
+        add_mask(0, 0)
         code_transposes(2, 0)
         code_transposes(2, 1)
         stage1(1, 0)
+        stage1(1, 1)
+        evacuate(1, 0)
         add_mask(0, 1)
-        scale_features(0)
         code_transposes(3, 0)
+        scale_features(0)
         coded_transposes(0)
-        code_transposes(3, 1)
         code_quantize(2)
-        stage1(2, 0)
+        code_transposes(3, 1)
         add_mask(1, 0)
-        stage1(2, 1)
+        stage1(2, 0)
         add_mask(1, 1)
         coded_quantize(0)
+        stage1(2, 1)
+        evacuate(2, 1)
         scale_features(1)
         add_mask(2, 0)
-        add_mask(2, 1)
         code_quantize(3)
+        add_mask(2, 1)
         stage2(0)
-        product(4)
         coded_transposes(1)
+        product(4)
         scale_features(2)
         coded_quantize(1)
 

@@ -16,212 +16,157 @@ FP8X4 = mybir.dt.float8_e4m3fn_x4
 FP4X4 = mybir.dt.float4_e2m1fn_x4
 ADD = mybir.AluOpType.add
 MULT = mybir.AluOpType.mult
-COPY = mybir.ActivationFunctionType.Copy
 
 P = 128
+PACK = 4
+K_PASS = P * PACK
+NH = 512
+FP4_BYTES = 2
+
 TILES = M // P
 PAIRS = TILES // 2
-NH = 512
-OLD_PASSES = K2 // 512
-PASSES = 1 + OLD_PASSES
-X_PASSES = F // 512
+HALVES = F // NH
+OLD_PASSES = K2 // K_PASS
+PASSES = (K1 + K2) // K_PASS
+X_PASSES = F // K_PASS
+X_BLOCKS = B // NH
 
 
 def tile_coded_worker_products_s3_kernel(
     tc, code_new, data_new, code_old_bytes, code_old_scale, old_words, old_scales, mask, feature_scale, x_words, x_scales, out
 ):
     nc = tc.nc
+    scalar_copy, vector_copy = nc.scalar.copy, nc.vector.tensor_copy
+
     with ExitStack() as ctx:
         keep = ctx.enter_context(tc.tile_pool(name="keep", bufs=1))
         work = ctx.enter_context(tc.tile_pool(name="work", bufs=3))
         psum = ctx.enter_context(tc.psum_pool(name="psum", bufs=1))
         ctx.enter_context(tc.manual_schedule())
 
-        warm = keep.tile([P, 8], F32)
-        nc.vector.memset(warm[:], 0.0)
-        o_sc = keep.tile([P, OLD_PASSES, F], U8, align_bytes=64)
-        x_sc = keep.tile([P, X_PASSES, B], U8, align_bytes=64)
-        nc.vector.memset(o_sc[:].rearrange("p g n -> p (g n)").bitcast(I32), 0)
-        nc.vector.memset(x_sc[:].rearrange("p g n -> p (g n)").bitcast(I32), 0)
+        old_plane = keep.tile([P, OLD_PASSES, F], U8, align_bytes=64)
+        x_plane = keep.tile([P, X_PASSES, B], U8, align_bytes=64)
+        primer = keep.tile([P, 2], F32)
+        nc.vector.memset(primer[:], 0.0)
+        nc.vector.memset(old_plane[:].rearrange("p g n -> p (g n)").bitcast(I32), 0)
+        nc.vector.memset(x_plane[:].rearrange("p g n -> p (g n)").bitcast(I32), 0)
 
         scale_cols = []
         for g in range(OLD_PASSES):
-            sc = keep.tile([P, 4], F32, name=f"scale_cols_{g}")
-            nc.scalar.dma_start(out=sc[:], in_=code_old_scale.rearrange("o (g p c) -> g p (o c)", p=P, c=4)[g])
-            scale_cols.append(sc)
-        fs_f32 = keep.tile([P, 2, 4], F32)
-        fs_cols = keep.tile([P, 2, 4], BF16)
-        nc.scalar.dma_start(out=fs_cols[:], in_=feature_scale.rearrange("(g p c) -> p g c", p=P, c=4))
-        nc.scalar.copy(out=warm[:, 1:2], in_=warm[:, 0:1])
+            cols = keep.tile([P, PACK], F32, name=f"scale_cols_{g}")
+            nc.scalar.dma_start(out=cols[:], in_=code_old_scale.rearrange("o (g p c) -> g p (o c)", p=P, c=PACK)[g])
+            scale_cols.append(cols)
+        feature_cols_f32 = keep.tile([P, HALVES, PACK], F32)
+        feature_cols = keep.tile([P, HALVES, PACK], BF16)
+        nc.scalar.dma_start(out=feature_cols[:], in_=feature_scale.rearrange("(g p c) -> p g c", p=P, c=PACK))
+        nc.scalar.copy(out=primer[:, 1:2], in_=primer[:, 0:1])
         ident = keep.tile([P, P], F32)
         make_identity(nc, ident[:])
 
-        old_v = code_old_bytes.rearrange("(j p i) k -> j p i k", p=P, i=2)
-        new_v = code_new.rearrange("(j p i) k -> j p i k", p=P, i=2)
-        mask_v = mask.rearrange("(j p i) f -> j p i f", p=P, i=2)
-        out_v = out.rearrange("(j p i) b -> j i p b", p=P, i=2)
+        old_rows = code_old_bytes.rearrange("(j p i) k -> j p i k", p=P, i=2)
+        new_rows = code_new.rearrange("(j p i) k -> j p i k", p=P, i=2)
+        mask_rows = mask.rearrange("(j p i) f -> j p i f", p=P, i=2)
+        out_rows = out.rearrange("(j p i) b -> j i p b", p=P, i=2)
 
-        old_tiles = []
-        new_tiles = []
+        old_bytes = []
+        code_rows = []
         mask_tiles = []
         for j in range(PAIRS):
             ob = keep.tile([P, 2, K2], U8, name=f"old_bytes_{j}")
-            nw = keep.tile([P, 2, K1], BF16, name=f"new_rows_{j}")
-            mk = keep.tile([P, 2, F], BF16, name=f"mask_rows_{j}")
-            old_tiles.append(ob)
-            new_tiles.append(nw)
+            cr = keep.tile([P, 2, K1 + K2], BF16, name=f"code_rows_{j}", align_bytes=64)
+            mk = keep.tile([P, 2, F], BF16, name=f"mask_{j}")
+            old_bytes.append(ob)
+            code_rows.append(cr)
             mask_tiles.append(mk)
-
-        data_raw = keep.tile([P, 4, F], BF16)
-        o_words = []
-        for h in range(2):
-            ow = keep.tile([P, OLD_PASSES, 2 * NH], U8, name=f"old_words_{h}", align_bytes=64)
-            o_words.append(ow)
-        x_w = []
+        data_raw = keep.tile([P, PACK, F], BF16)
+        old_code = []
+        for h in range(HALVES):
+            oc = keep.tile([P, OLD_PASSES, FP4_BYTES * NH], U8, name=f"old_code_{h}", align_bytes=64)
+            old_code.append(oc)
+        x_code = []
         for g in range(X_PASSES):
-            xw = keep.tile([P, 2 * B], U8, name=f"x_words_{g}", align_bytes=64)
-            x_w.append(xw)
+            xc = keep.tile([P, FP4_BYTES * B], U8, name=f"x_code_{g}", align_bytes=64)
+            x_code.append(xc)
 
-        def load_data():
-            nc.sync.dma_start(out=data_raw[:], in_=data_new.rearrange("(p t) f -> p t f", t=4))
-
-        def load_old_words(h):
-            nc.sync.dma_start(out=o_words[h][:], in_=old_words.rearrange("g p n -> p g n")[:, :, 2 * NH * h : 2 * NH * (h + 1)])
-
-        def load_scales(tile, src):
-            for q in range(4):
-                nc.sync.dma_start(
-                    out=tile[32 * q : 32 * q + 4, :, :].bitcast(I32),
-                    in_=src.rearrange("g q n -> q g n")[4 * q : 4 * q + 4, :, :].bitcast(I32),
-                )
-
-        def load_x(g):
-            nc.sync.dma_start(out=x_w[g][:], in_=x_words[g])
+        def load_first_pair(i):
+            nc.sync.dma_start(out=old_bytes[0][:, i, :], in_=old_rows[0, :, i, :])
+            nc.sync.dma_start(out=code_rows[0][:, i, 0:K1], in_=new_rows[0, :, i, :])
 
         def load_old_pair(j):
-            nc.sync.dma_start(out=old_tiles[j][:], in_=old_v[j])
+            nc.sync.dma_start(out=old_bytes[j][:], in_=old_rows[j])
 
         def load_new_pair(j):
-            nc.sync.dma_start(out=new_tiles[j][:], in_=new_v[j])
+            nc.sync.dma_start(out=code_rows[j][:, :, 0:K1], in_=new_rows[j])
 
         def load_mask(j):
-            nc.sync.dma_start(out=mask_tiles[j][:], in_=mask_v[j])
+            nc.sync.dma_start(out=mask_tiles[j][:], in_=mask_rows[j])
 
-        def load_codes(i):
-            nc.sync.dma_start(out=old_tiles[0][:, i, :], in_=old_v[0, :, i, :])
-            nc.sync.dma_start(out=new_tiles[0][:, i, :], in_=new_v[0, :, i, :])
+        def load_old_code(h):
+            cols = slice(FP4_BYTES * NH * h, FP4_BYTES * NH * (h + 1))
+            nc.sync.dma_start(out=old_code[h][:], in_=old_words.rearrange("g p n -> p g n")[:, :, cols])
 
-        load_codes(0)
-        load_data()
-        load_codes(1)
+        def load_x_code(g):
+            nc.sync.dma_start(out=x_code[g][:], in_=x_words[g])
+
+        def load_scales(plane, source):
+            for q in range(4):
+                nc.sync.dma_start(
+                    out=plane[32 * q : 32 * q + 4, :, :].bitcast(I32),
+                    in_=source.rearrange("g q n -> q g n")[4 * q : 4 * q + 4, :, :].bitcast(I32),
+                )
+
+        load_first_pair(0)
+        nc.sync.dma_start(out=data_raw[:], in_=data_new.rearrange("(p t) f -> p t f", t=PACK))
+        load_first_pair(1)
         load_old_pair(1)
-        load_old_words(0)
-        load_scales(o_sc, old_scales)
-        load_old_words(1)
+        load_scales(old_plane, old_scales)
         load_new_pair(1)
+        load_old_code(0)
+        load_old_code(1)
         load_mask(0)
-        load_mask(1)
-        load_new_pair(2)
-        load_x(0)
-        load_scales(x_sc, x_scales)
-        load_x(1)
+        load_x_code(0)
         load_old_pair(2)
+        load_new_pair(2)
+        load_x_code(1)
+        load_scales(x_plane, x_scales)
+        load_mask(1)
+        load_old_pair(3)
         load_new_pair(3)
         load_mask(2)
         load_mask(3)
-        load_old_pair(3)
-        scale_all = keep.tile([P, K2], F32)
-        fs_all = keep.tile([P, F], F32)
 
-        def spread_features(h):
-            bank = psum.tile([P, 4, P], F32, name=f"fs_{h}", tag="tr", bufs=2)
-            spread(bank, fs_f32[:, h, :])
-            unspread(nc.scalar.copy, fs_all[:, NH * h : NH * (h + 1)], bank)
+        scale_all = keep.tile([P, K2], F32)
+        feature_all = keep.tile([P, F], F32)
 
         def spread(bank, cols):
-            for c in range(4):
+            for c in range(PACK):
                 nc.tensor.transpose(bank[:, c, :], cols[:, c : c + 1].to_broadcast([P, P]), ident[:])
 
-        def unspread(copy, dst, bank):
-            copy(out=dst.rearrange("p (n c) -> p n c", c=4), in_=bank[:].rearrange("p c n -> p n c"))
+        def collect(dst, bank):
+            nc.scalar.copy(out=dst.rearrange("p (n c) -> p n c", c=PACK), in_=bank[:].rearrange("p c n -> p n c"))
 
-        sp0 = psum.tile([P, 4, P], F32, name="sp0", tag="tr", bufs=2)
-        spread(sp0, scale_cols[0])
-        sp1 = psum.tile([P, 4, P], F32, name="sp1", tag="tr", bufs=2)
-        spread(sp1, scale_cols[1])
-        sp2 = psum.tile([P, 4, P], F32, name="sp2", tag="trc", bufs=1)
-        spread(sp2, scale_cols[2])
-        unspread(nc.scalar.copy, scale_all[:, 0:512], sp0)
-        unspread(nc.scalar.copy, scale_all[:, 512:1024], sp1)
-        unspread(nc.scalar.copy, scale_all[:, 1024:1536], sp2)
-        nc.scalar.copy(out=fs_f32[:], in_=fs_cols[:])
+        scale_banks = []
+        for g in range(OLD_PASSES):
+            if g < 2:
+                bank = psum.tile([P, PACK, P], F32, name=f"scale_bank_{g}", tag="code_bank", bufs=2)
+            else:
+                bank = psum.tile([P, PACK, P], F32, name=f"scale_bank_{g}", tag="coded_bank", bufs=1)
+            spread(bank, scale_cols[g])
+            scale_banks.append(bank)
+        for g in range(OLD_PASSES):
+            collect(scale_all[:, K_PASS * g : K_PASS * (g + 1)], scale_banks[g])
+        nc.scalar.copy(out=feature_cols_f32[:], in_=feature_cols[:])
 
-        prods = {}
-        groups = {}
-        kcodes = {}
-        sums = {}
-        cs = {}
-        cgroups = {}
-        ccodes = {}
-
-        def product(t, g0=0, g1=OLD_PASSES):
-            if g0 == 0:
-                pr = work.tile([P, K2], BF16, name=f"prod_{t}", tag="prod", bufs=3, align_bytes=64)
-                prods[t] = pr
-            k = slice(512 * g0, 512 * g1)
-            nc.vector.tensor_tensor(
-                out=prods[t][:, k], in0=old_tiles[t // 2][:, t % 2, k].bitcast(FP8), in1=scale_all[:, k], op=MULT
-            )
-
-        perms = {}
-
-        def permute(t):
-            pm = work.tile([P, PASSES, 2, P], F32, name=f"perm_{t}", tag="perm", bufs=2)
-            nc.scalar.copy(out=pm[:, 0, :, :], in_=new_tiles[t // 2][:, t % 2, :].bitcast(F32).rearrange("p (w u) -> p u w", u=2))
-            nc.scalar.copy(out=pm[:, 1:, :, :], in_=prods[t][:].bitcast(F32).rearrange("p (g w u) -> p g u w", g=OLD_PASSES, u=2))
-            perms[t] = pm
-
-        def warm_up(n):
-            bank = psum.tile([P, NH], F32, name="warm_bank", tag="acc", bufs=5)
-            for k in range(n):
-                nc.tensor.matmul(bank[:], lhsT=new_tiles[0][:, 0, 0:P], rhs=new_tiles[0][:, 0, :], start=True, stop=True)
-
-        def code_transposes(t, half):
-            bank = psum.tile([P, 2, 2, P], F32, name=f"tr_{t}_{half}", tag="tr", bufs=2)
-            for s in range(2):
-                g = 2 * half + s
-                for u in range(2):
-                    if t not in perms:
-                        words = new_tiles[t // 2][:, t % 2, :].bitcast(F32) if g == 0 else prods[t][:, 512 * (g - 1) : 512 * g].bitcast(F32)
-                        words = words[:, u : 256 : 2]
-                    else:
-                        words = perms[t][:, g, u, :]
-                    nc.tensor.transpose(bank[:, s, u, :], words, ident[:])
-            if half == 0:
-                gr = work.tile([P, PASSES, P, 4], BF16, name=f"grouped_{t}", tag="grouped", bufs=3, align_bytes=64)
-                groups[t] = gr
-            nc.scalar.copy(
-                out=groups[t][:, 2 * half : 2 * half + 2, :, :].bitcast(F32), in_=bank[:].rearrange("p s u m -> p s m u")
-            )
-
-        def code_quantize(t, g0=0, g1=PASSES):
-            if g0 == 0:
-                kc = work.tile([P, PASSES, P], U32, name=f"kcodes_{t}", tag="kcodes", bufs=3, align_bytes=64)
-                ks = work.tile([P, PASSES, P], U8, name=f"kscales_{t}", tag="kscales", bufs=3, align_bytes=64)
-                kcodes[t] = (kc, ks)
-            kc, ks = kcodes[t]
-            s = slice(g0, g1)
-            nc.vector.quantize_mx(
-                out=kc[:, s, :].rearrange("p s m -> p (s m)").bitcast(FP8X4),
-                scales=ks[:, s, :].rearrange("p s m -> p (s m)"),
-                in_=groups[t][:, s, :, :].rearrange("p s m t -> p (s m t)"),
-            )
+        def spread_features(h):
+            bank = psum.tile([P, PACK, P], F32, name=f"feature_bank_{h}", tag="code_bank", bufs=2)
+            spread(bank, feature_cols_f32[:, h, :])
+            collect(feature_all[:, NH * h : NH * (h + 1)], bank)
 
         data_grouped = []
         data_codes = []
         data_scales = []
-        for h in range(2):
-            dg = keep.tile([P, NH, 4], BF16, name=f"data_grouped_{h}", align_bytes=64)
+        for h in range(HALVES):
+            dg = keep.tile([P, NH, PACK], BF16, name=f"data_grouped_{h}", align_bytes=64)
             dc = keep.tile([P, NH], U32, name=f"data_codes_{h}", align_bytes=64)
             ds = keep.tile([P, NH], U8, name=f"data_scales_{h}", align_bytes=64)
             data_grouped.append(dg)
@@ -229,7 +174,8 @@ def tile_coded_worker_products_s3_kernel(
             data_scales.append(ds)
 
         def data_interleave(copy, h, n0, n1):
-            copy(out=data_grouped[h][:, n0:n1, :], in_=data_raw[:, :, NH * h + n0 : NH * h + n1].rearrange("p t n -> p n t"))
+            source = data_raw[:, :, NH * h + n0 : NH * h + n1]
+            copy(out=data_grouped[h][:, n0:n1, :], in_=source.rearrange("p t n -> p n t"))
 
         def data_quantize(h):
             nc.vector.quantize_mx(
@@ -238,178 +184,227 @@ def tile_coded_worker_products_s3_kernel(
                 in_=data_grouped[h][:].rearrange("p n t -> p (n t)"),
             )
 
-        def stage1(t, h):
-            acc = psum.tile([P, NH], F32, name=f"acc1_{t}_{h}", tag="acc", bufs=5)
-            kc, ks = kcodes[t]
-            order = [1, 2, 3, 0] if h == 1 else [1, 0, 2, 3]
+        permuted = {}
+        grouped = {}
+        code_ops = {}
+        sums = {}
+        masked = {}
+        coded = {}
+        coded_grouped = {}
+        coded_ops = {}
+
+        def product(tile, g0=0, g1=OLD_PASSES):
+            k = slice(K_PASS * g0, K_PASS * g1)
+            nc.vector.tensor_tensor(
+                out=code_rows[tile // 2][:, tile % 2, K1 + K_PASS * g0 : K1 + K_PASS * g1],
+                in0=old_bytes[tile // 2][:, tile % 2, k].bitcast(FP8),
+                in1=scale_all[:, k],
+                op=MULT,
+            )
+
+        def permute(tile):
+            pm = work.tile([P, PASSES, 2, P], F32, name=f"permuted_{tile}", tag="permuted", bufs=3)
+            words = code_rows[tile // 2][:, tile % 2, :].bitcast(F32)
+            nc.scalar.copy(out=pm[:], in_=words.rearrange("p (g w u) -> p g u w", g=PASSES, u=2))
+            permuted[tile] = pm
+
+        def code_transposes(tile):
+            gr = work.tile([P, PASSES, P, PACK], BF16, name=f"grouped_{tile}", tag="grouped", bufs=3, align_bytes=64)
+            grouped[tile] = gr
+            for g0 in (0, 2):
+                bank = psum.tile([P, 2, 2, P], F32, name=f"code_bank_{tile}_{g0}", tag="code_bank", bufs=2)
+                for s in range(2):
+                    g = g0 + s
+                    for u in range(2):
+                        if tile in permuted:
+                            words = permuted[tile][:, g, u, :]
+                        else:
+                            row = code_rows[tile // 2][:, tile % 2, K_PASS * g : K_PASS * (g + 1)]
+                            words = row.bitcast(F32)[:, u : K_PASS // 2 : 2]
+                        nc.tensor.transpose(bank[:, s, u, :], words, ident[:])
+                nc.scalar.copy(out=gr[:, g0 : g0 + 2, :, :].bitcast(F32), in_=bank[:].rearrange("p s u m -> p s m u"))
+
+        def code_quantize(tile, g0=0, g1=PASSES):
+            if g0 == 0:
+                codes = work.tile([P, PASSES, P], U32, name=f"code_codes_{tile}", tag="code_codes", bufs=3, align_bytes=64)
+                scales = work.tile([P, PASSES, P], U8, name=f"code_scales_{tile}", tag="code_scales", bufs=3, align_bytes=64)
+                code_ops[tile] = (codes, scales)
+            codes, scales = code_ops[tile]
+            nc.vector.quantize_mx(
+                out=codes[:, g0:g1, :].rearrange("p g m -> p (g m)").bitcast(FP8X4),
+                scales=scales[:, g0:g1, :].rearrange("p g m -> p (g m)"),
+                in_=grouped[tile][:, g0:g1, :, :].rearrange("p g m t -> p (g m t)"),
+            )
+
+        def stage1(tile, h):
+            acc = psum.tile([P, NH], F32, name=f"stage1_{tile}_{h}", tag="acc", bufs=5)
+            codes, scales = code_ops[tile]
+            order = [1, 0, 2, 3] if h == 0 else [1, 2, 3, 0]
             for n, g in enumerate(order):
-                rhs = data_codes[h][:].bitcast(FP8X4) if g == 0 else o_words[h][:, g - 1, :].bitcast(FP4X4)
-                rhs_scale = data_scales[h][:] if g == 0 else o_sc[:, g - 1, NH * h : NH * (h + 1)]
+                if g == 0:
+                    rhs = data_codes[h][:].bitcast(FP8X4)
+                    rhs_scale = data_scales[h][:]
+                else:
+                    rhs = old_code[h][:, g - 1, :].bitcast(FP4X4)
+                    rhs_scale = old_plane[:, g - 1, NH * h : NH * (h + 1)]
                 nc.tensor.matmul_mx(
                     out=acc[:],
-                    lhsT=kc[:, g, :].bitcast(FP8X4),
-                    lhsT_scale=ks[:, g, :],
+                    lhsT=codes[:, g, :].bitcast(FP8X4),
+                    lhsT_scale=scales[:, g, :],
                     rhs=rhs,
                     rhs_scale=rhs_scale,
                     start=(n == 0),
                     stop=(n == PASSES - 1),
                 )
-            sums[t, h] = acc
+            sums[tile, h] = acc
 
-        def evacuate(t, h):
-            ev = work.tile([P, NH], F32, name=f"evac_{t}_{h}", tag="evac", bufs=6)
-            nc.scalar.copy(out=ev[:], in_=sums[t, h][:])
-            sums[t, h] = ev
+        def evacuate(tile, h):
+            copy = work.tile([P, NH], F32, name=f"sum_{tile}_{h}", tag="sum", bufs=1)
+            nc.scalar.copy(out=copy[:], in_=sums[tile, h][:])
+            sums[tile, h] = copy
 
-        def add_mask(t, h):
+        def add_mask(tile, h):
             if h == 0:
-                s = work.tile([P, F], F32, name=f"masked_{t}", tag="masked", bufs=2)
-                cs[t] = s
+                mt = work.tile([P, F], F32, name=f"masked_{tile}", tag="masked", bufs=2)
+                masked[tile] = mt
             cols = slice(NH * h, NH * (h + 1))
-            nc.vector.tensor_tensor(out=cs[t][:, cols], in0=sums[t, h][:], in1=mask_tiles[t // 2][:, t % 2, cols], op=ADD)
+            nc.vector.tensor_tensor(
+                out=masked[tile][:, cols], in0=sums[tile, h][:], in1=mask_tiles[tile // 2][:, tile % 2, cols], op=ADD
+            )
 
-        def scale_features(t):
-            c = work.tile([P, 2, 2 * P, 2], BF16, name=f"coded_{t}", tag="coded", bufs=2, align_bytes=64)
+        def scale_features(tile):
+            c = work.tile([P, 2, F // PACK, 2], BF16, name=f"coded_{tile}", tag="coded", bufs=2, align_bytes=64)
             nc.vector.tensor_tensor(
                 out=c[:],
-                in0=cs[t][:].rearrange("p (w u e) -> p u w e", u=2, e=2),
-                in1=fs_all[:].rearrange("p (w u e) -> p u w e", u=2, e=2),
+                in0=masked[tile][:].rearrange("p (w u e) -> p u w e", u=2, e=2),
+                in1=feature_all[:].rearrange("p (w u e) -> p u w e", u=2, e=2),
                 op=MULT,
             )
-            cs[t] = c
+            coded[tile] = c
 
-        def coded_early(t, h):
-            bank = psum.tile([P, 4, P], F32, name=f"tre_{t}_{h}", tag="trc", bufs=1)
-            if h == 0:
-                cg = work.tile([P, 2, P, 4], BF16, name=f"coded_grouped_{t}", tag="coded_grouped", bufs=2, align_bytes=64)
-                cgroups[t] = cg
-            for c in range(4):
-                nc.tensor.transpose(bank[:, c, :], cs[t][:, NH * h + c : NH * (h + 1) : 4], ident[:])
-            for c in range(4):
-                nc.scalar.activation(out=cgroups[t][:, h, :, c], in_=bank[:, c, :], func=COPY, scale=fs_f32[:, h, c : c + 1])
-
-        def coded_transposes(t):
-            bank = psum.tile([P, 2, 2, P], F32, name=f"trc_{t}", tag="trc", bufs=1)
-            words = cs[t][:].rearrange("p u w e -> p (u w e)").bitcast(F32)
-            for h in range(2):
+        def coded_transposes(copy, tile):
+            bank = psum.tile([P, X_PASSES, 2, P], F32, name=f"coded_bank_{tile}", tag="coded_bank", bufs=1)
+            words = coded[tile][:].rearrange("p u w e -> p (u w e)").bitcast(F32)
+            for g in range(X_PASSES):
                 for u in range(2):
-                    nc.tensor.transpose(bank[:, h, u, :], words[:, 2 * P * u + P * h : 2 * P * u + P * (h + 1)], ident[:])
-            cg = work.tile([P, 2, P, 4], BF16, name=f"coded_grouped_{t}", tag="coded_grouped", bufs=2, align_bytes=64)
-            nc.scalar.copy(out=cg[:].bitcast(F32), in_=bank[:].rearrange("p h u m -> p h m u"))
-            cgroups[t] = cg
+                    first = (X_PASSES * u + g) * P
+                    nc.tensor.transpose(bank[:, g, u, :], words[:, first : first + P], ident[:])
+            cg = work.tile([P, X_PASSES, P, PACK], BF16, name=f"coded_grouped_{tile}", tag="coded_grouped", bufs=2, align_bytes=64)
+            copy(out=cg[:].bitcast(F32), in_=bank[:].rearrange("p g u m -> p g m u"))
+            coded_grouped[tile] = cg
 
-        def coded_quantize(t):
-            cc = work.tile([P, 2, P], U32, name=f"ccodes_{t}", tag="ccodes", bufs=2, align_bytes=64)
-            cz = work.tile([P, 2, P], U8, name=f"cscales_{t}", tag="cscales", bufs=2, align_bytes=64)
+        def coded_quantize(tile):
+            codes = work.tile([P, X_PASSES, P], U32, name=f"coded_codes_{tile}", tag="coded_codes", bufs=2, align_bytes=64)
+            scales = work.tile([P, X_PASSES, P], U8, name=f"coded_scales_{tile}", tag="coded_scales", bufs=2, align_bytes=64)
             nc.vector.quantize_mx(
-                out=cc[:].rearrange("p h m -> p (h m)").bitcast(FP8X4),
-                scales=cz[:].rearrange("p h m -> p (h m)"),
-                in_=cgroups[t][:].rearrange("p h m t -> p (h m t)"),
+                out=codes[:].rearrange("p g m -> p (g m)").bitcast(FP8X4),
+                scales=scales[:].rearrange("p g m -> p (g m)"),
+                in_=coded_grouped[tile][:].rearrange("p g m t -> p (g m t)"),
             )
-            ccodes[t] = (cc, cz)
+            coded_ops[tile] = (codes, scales)
 
-        def stage2(t):
-            cc, cz = ccodes[t]
-            res = work.tile([P, B], F32, name=f"result_{t}", tag="result", bufs=3)
-            for b in range(B // NH):
-                acc = psum.tile([P, NH], F32, name=f"acc2_{t}_{b}", tag="acc", bufs=5)
+        def stage2(tile, on_vector=()):
+            codes, scales = coded_ops[tile]
+            result = work.tile([P, B], F32, name=f"result_{tile}", tag="result", bufs=3)
+            blocks = 1 if tile == TILES - 1 else 2
+            for b in range(X_BLOCKS):
+                cols = slice(NH * b, NH * (b + 1))
+                acc = psum.tile([P, NH], F32, name=f"stage2_{tile}_{b}", tag="acc", bufs=5)
                 for g in range(X_PASSES):
                     nc.tensor.matmul_mx(
                         out=acc[:],
-                        lhsT=cc[:, g, :].bitcast(FP8X4),
-                        lhsT_scale=cz[:, g, :],
-                        rhs=x_w[g][:, 2 * NH * b : 2 * NH * (b + 1)].bitcast(FP4X4),
-                        rhs_scale=x_sc[:, g, NH * b : NH * (b + 1)],
+                        lhsT=codes[:, g, :].bitcast(FP8X4),
+                        lhsT_scale=scales[:, g, :],
+                        rhs=x_code[g][:, FP4_BYTES * NH * b : FP4_BYTES * NH * (b + 1)].bitcast(FP4X4),
+                        rhs_scale=x_plane[:, g, cols],
                         start=(g == 0),
                         stop=(g == X_PASSES - 1),
                     )
-                last = t == TILES - 1
-                if last and b == B // NH - 1:
-                    nc.scalar.copy(out=res[:, NH * b : NH * b + NH // 2], in_=acc[:, : NH // 2])
-                    nc.vector.tensor_copy(out=res[:, NH * b + NH // 2 : NH * (b + 1)], in_=acc[:, NH // 2 :])
-                elif t >= TILES - 2 and b % 2 == 0:
-                    nc.vector.tensor_copy(out=res[:, NH * b : NH * (b + 1)], in_=acc[:])
-                else:
-                    nc.scalar.copy(out=res[:, NH * b : NH * (b + 1)], in_=acc[:])
-                if last or b % 2 == 1:
-                    cols = slice(NH * b, NH * (b + 1)) if last else slice(NH * (b - 1), NH * (b + 1))
-                    nc.sync.dma_start(out=out_v[t // 2, t % 2, :, cols], in_=res[:, cols])
+                copy = vector_copy if b in on_vector else scalar_copy
+                copy(out=result[:, cols], in_=acc[:])
+                if (b + 1) % blocks == 0:
+                    stored = slice(NH * (b + 1 - blocks), NH * (b + 1))
+                    nc.sync.dma_start(out=out_rows[tile // 2, tile % 2, :, stored], in_=result[:, stored])
 
-        product(0, 0, 1)
-        code_transposes(0, 0)
+        def warm_up(count):
+            bank = psum.tile([P, NH], F32, name="warm_up", tag="acc", bufs=5)
+            rows = code_rows[0][:, 0, 0:NH]
+            for n in range(count):
+                nc.tensor.matmul(bank[:], lhsT=rows[:, 0:P], rhs=rows, start=True, stop=True)
+
+        for g in range(OLD_PASSES):
+            product(0, g, g + 1)
+        code_transposes(0)
+        data_interleave(scalar_copy, 0, 0, NH // 2)
+        data_interleave(vector_copy, 0, NH // 2, NH)
         spread_features(0)
-        product(0, 1, 2)
-        product(0, 2, 3)
-        data_interleave(nc.vector.tensor_copy, 0, 128, 512)
-        data_interleave(nc.scalar.copy, 0, 0, 128)
-        code_transposes(0, 1)
-        product(1)
-        data_quantize(0)
         spread_features(1)
-        code_quantize(0, 0, 2)
-        data_interleave(nc.scalar.copy, 1, 0, 384)
-        code_quantize(0, 2, 4)
+        product(1)
         warm_up(6)
-        code_transposes(1, 0)
-        data_interleave(nc.vector.tensor_copy, 1, 384, 512)
-        product(2)
-        code_transposes(1, 1)
-        stage1(0, 0)
-        data_quantize(1)
-        code_quantize(1)
+        data_interleave(scalar_copy, 1, 0, NH)
+        code_transposes(1)
         product(3)
-        stage1(0, 1)
-        evacuate(0, 0)
+        code_quantize(0, 0, 2)
+        code_quantize(0, 2, 4)
+        data_quantize(0)
         permute(3)
+        product(2)
+        data_quantize(1)
+        stage1(0, 0)
+        stage1(0, 1)
         add_mask(0, 0)
-        code_transposes(2, 0)
-        code_transposes(2, 1)
+        code_quantize(1)
+        code_transposes(2)
         stage1(1, 0)
         stage1(1, 1)
-        evacuate(1, 0)
         add_mask(0, 1)
-        code_transposes(3, 0)
         scale_features(0)
-        coded_transposes(0)
         code_quantize(2)
-        code_transposes(3, 1)
+        coded_transposes(scalar_copy, 0)
+        code_transposes(3)
         add_mask(1, 0)
-        stage1(2, 0)
         add_mask(1, 1)
-        coded_quantize(0)
         stage1(2, 1)
-        evacuate(2, 1)
-        scale_features(1)
-        add_mask(2, 0)
-        code_quantize(3)
-        add_mask(2, 1)
-        stage2(0)
-        coded_transposes(1)
         product(4)
+        coded_quantize(0)
+        stage1(2, 0)
+        scale_features(1)
+        code_quantize(3)
+        evacuate(2, 1)
+        add_mask(2, 0)
+        permute(4)
+        add_mask(2, 1)
+        stage2(0, on_vector=(3,))
+        coded_transposes(scalar_copy, 1)
         scale_features(2)
         coded_quantize(1)
 
-        for i in range(3, TILES):
-            if i + 1 < TILES:
-                permute(i + 1)
+        for i in range(3, TILES - 1):
             stage1(i, 0)
-            stage1(i, 1)
+            add_mask(i, 0)
+            code_transposes(i + 1)
             if i + 2 < TILES:
                 product(i + 2)
-            add_mask(i, 0)
+            coded_transposes(scalar_copy, i - 1)
+            stage1(i, 1)
+            code_quantize(i + 1)
             add_mask(i, 1)
-            coded_transposes(i - 1)
-            if i + 1 < TILES:
-                code_transposes(i + 1, 0)
-                code_transposes(i + 1, 1)
-                coded_quantize(i - 1)
-                code_quantize(i + 1)
-                scale_features(i)
-            else:
-                scale_features(i)
-                coded_quantize(i - 1)
+            if i + 2 < TILES:
+                permute(i + 2)
             stage2(i - 2)
-        coded_transposes(TILES - 1)
-        coded_quantize(TILES - 1)
-        stage2(TILES - 2)
-        stage2(TILES - 1)
+            coded_quantize(i - 1)
+            scale_features(i)
+
+        last = TILES - 1
+        stage1(last, 0)
+        stage1(last, 1)
+        coded_transposes(scalar_copy, last - 1)
+        add_mask(last, 0)
+        add_mask(last, 1)
+        scale_features(last)
+        stage2(last - 2)
+        coded_quantize(last - 1)
+        coded_transposes(vector_copy, last)
+        coded_quantize(last)
+        stage2(last - 1, on_vector=(2,))
+        stage2(last, on_vector=(2,))

from contextlib import ExitStack

import concourse.mybir as mybir
from concourse.masks import make_identity

M, K1, K2, F, B = 1024, 512, 1536, 1024, 2048
FLOPS = 2 * M * (K1 + K2) * F + 2 * M * F * B

F32 = mybir.dt.float32
BF16 = mybir.dt.bfloat16
I32 = mybir.dt.int32
U32 = mybir.dt.uint32
U8 = mybir.dt.uint8
FP8 = mybir.dt.float8_e4m3fn
FP8X4 = mybir.dt.float8_e4m3fn_x4
FP4X4 = mybir.dt.float4_e2m1fn_x4
ADD = mybir.AluOpType.add
MULT = mybir.AluOpType.mult

P = 128
PACK = 4
K_PASS = P * PACK
NH = 512
FP4_BYTES = 2

TILES = M // P
PAIRS = TILES // 2
HALVES = F // NH
OLD_PASSES = K2 // K_PASS
PASSES = (K1 + K2) // K_PASS
X_PASSES = F // K_PASS
X_BLOCKS = B // NH


def tile_coded_worker_products_s3_kernel(
    tc, code_new, data_new, code_old_bytes, code_old_scale, old_words, old_scales, mask, feature_scale, x_words, x_scales, out
):
    nc = tc.nc
    scalar_copy, vector_copy = nc.scalar.copy, nc.vector.tensor_copy

    with ExitStack() as ctx:
        keep = ctx.enter_context(tc.tile_pool(name="keep", bufs=1))
        work = ctx.enter_context(tc.tile_pool(name="work", bufs=3))
        psum = ctx.enter_context(tc.psum_pool(name="psum", bufs=1))
        ctx.enter_context(tc.manual_schedule())

        old_plane = keep.tile([P, OLD_PASSES, F], U8, align_bytes=64)
        x_plane = keep.tile([P, X_PASSES, B], U8, align_bytes=64)
        primer = keep.tile([P, 2], F32)
        nc.vector.memset(primer[:], 0.0)
        nc.vector.memset(old_plane[:].rearrange("p g n -> p (g n)").bitcast(I32), 0)
        nc.vector.memset(x_plane[:].rearrange("p g n -> p (g n)").bitcast(I32), 0)

        scale_cols = []
        for g in range(OLD_PASSES):
            cols = keep.tile([P, PACK], F32, name=f"scale_cols_{g}")
            nc.scalar.dma_start(out=cols[:], in_=code_old_scale.rearrange("o (g p c) -> g p (o c)", p=P, c=PACK)[g])
            scale_cols.append(cols)
        feature_cols_f32 = keep.tile([P, HALVES, PACK], F32)
        feature_cols = keep.tile([P, HALVES, PACK], BF16)
        nc.scalar.dma_start(out=feature_cols[:], in_=feature_scale.rearrange("(g p c) -> p g c", p=P, c=PACK))
        nc.scalar.copy(out=primer[:, 1:2], in_=primer[:, 0:1])
        ident = keep.tile([P, P], F32)
        make_identity(nc, ident[:])

        old_rows = code_old_bytes.rearrange("(j p i) k -> j p i k", p=P, i=2)
        new_rows = code_new.rearrange("(j p i) k -> j p i k", p=P, i=2)
        mask_rows = mask.rearrange("(j p i) f -> j p i f", p=P, i=2)
        out_rows = out.rearrange("(j p i) b -> j i p b", p=P, i=2)

        old_bytes = []
        code_rows = []
        mask_tiles = []
        for j in range(PAIRS):
            ob = keep.tile([P, 2, K2], U8, name=f"old_bytes_{j}")
            cr = keep.tile([P, 2, K1 + K2], BF16, name=f"code_rows_{j}", align_bytes=64)
            mk = keep.tile([P, 2, F], BF16, name=f"mask_{j}")
            old_bytes.append(ob)
            code_rows.append(cr)
            mask_tiles.append(mk)
        data_raw = keep.tile([P, PACK, F], BF16)
        old_code = []
        for h in range(HALVES):
            oc = keep.tile([P, OLD_PASSES, FP4_BYTES * NH], U8, name=f"old_code_{h}", align_bytes=64)
            old_code.append(oc)
        x_code = []
        for g in range(X_PASSES):
            xc = keep.tile([P, FP4_BYTES * B], U8, name=f"x_code_{g}", align_bytes=64)
            x_code.append(xc)

        def load_first_pair(i):
            nc.sync.dma_start(out=old_bytes[0][:, i, :], in_=old_rows[0, :, i, :])
            nc.sync.dma_start(out=code_rows[0][:, i, 0:K1], in_=new_rows[0, :, i, :])

        def load_old_pair(j):
            nc.sync.dma_start(out=old_bytes[j][:], in_=old_rows[j])

        def load_new_pair(j):
            nc.sync.dma_start(out=code_rows[j][:, :, 0:K1], in_=new_rows[j])

        def load_mask(j):
            nc.sync.dma_start(out=mask_tiles[j][:], in_=mask_rows[j])

        def load_old_code(h):
            cols = slice(FP4_BYTES * NH * h, FP4_BYTES * NH * (h + 1))
            nc.sync.dma_start(out=old_code[h][:], in_=old_words.rearrange("g p n -> p g n")[:, :, cols])

        def load_x_code(g):
            nc.sync.dma_start(out=x_code[g][:], in_=x_words[g])

        def load_scales(plane, source):
            for q in range(4):
                nc.sync.dma_start(
                    out=plane[32 * q : 32 * q + 4, :, :].bitcast(I32),
                    in_=source.rearrange("g q n -> q g n")[4 * q : 4 * q + 4, :, :].bitcast(I32),
                )

        load_first_pair(0)
        nc.sync.dma_start(out=data_raw[:], in_=data_new.rearrange("(p t) f -> p t f", t=PACK))
        load_first_pair(1)
        load_old_pair(1)
        load_scales(old_plane, old_scales)
        load_new_pair(1)
        load_old_code(0)
        load_old_code(1)
        load_mask(0)
        load_x_code(0)
        load_old_pair(2)
        load_new_pair(2)
        load_x_code(1)
        load_scales(x_plane, x_scales)
        load_mask(1)
        load_old_pair(3)
        load_new_pair(3)
        load_mask(2)
        load_mask(3)

        scale_all = keep.tile([P, K2], F32)
        feature_all = keep.tile([P, F], F32)

        def spread(bank, cols):
            for c in range(PACK):
                nc.tensor.transpose(bank[:, c, :], cols[:, c : c + 1].to_broadcast([P, P]), ident[:])

        def collect(dst, bank):
            nc.scalar.copy(out=dst.rearrange("p (n c) -> p n c", c=PACK), in_=bank[:].rearrange("p c n -> p n c"))

        scale_banks = []
        for g in range(OLD_PASSES):
            if g < 2:
                bank = psum.tile([P, PACK, P], F32, name=f"scale_bank_{g}", tag="code_bank", bufs=2)
            else:
                bank = psum.tile([P, PACK, P], F32, name=f"scale_bank_{g}", tag="coded_bank", bufs=1)
            spread(bank, scale_cols[g])
            scale_banks.append(bank)
        for g in range(OLD_PASSES):
            collect(scale_all[:, K_PASS * g : K_PASS * (g + 1)], scale_banks[g])
        nc.scalar.copy(out=feature_cols_f32[:], in_=feature_cols[:])

        def spread_features(h):
            bank = psum.tile([P, PACK, P], F32, name=f"feature_bank_{h}", tag="code_bank", bufs=2)
            spread(bank, feature_cols_f32[:, h, :])
            collect(feature_all[:, NH * h : NH * (h + 1)], bank)

        data_grouped = []
        data_codes = []
        data_scales = []
        for h in range(HALVES):
            dg = keep.tile([P, NH, PACK], BF16, name=f"data_grouped_{h}", align_bytes=64)
            dc = keep.tile([P, NH], U32, name=f"data_codes_{h}", align_bytes=64)
            ds = keep.tile([P, NH], U8, name=f"data_scales_{h}", align_bytes=64)
            data_grouped.append(dg)
            data_codes.append(dc)
            data_scales.append(ds)

        def data_interleave(copy, h, n0, n1):
            source = data_raw[:, :, NH * h + n0 : NH * h + n1]
            copy(out=data_grouped[h][:, n0:n1, :], in_=source.rearrange("p t n -> p n t"))

        def data_quantize(h):
            nc.vector.quantize_mx(
                out=data_codes[h][:].bitcast(FP8X4),
                scales=data_scales[h][:],
                in_=data_grouped[h][:].rearrange("p n t -> p (n t)"),
            )

        permuted = {}
        grouped = {}
        code_ops = {}
        sums = {}
        masked = {}
        coded = {}
        coded_grouped = {}
        coded_ops = {}

        def product(tile, g0=0, g1=OLD_PASSES):
            k = slice(K_PASS * g0, K_PASS * g1)
            nc.vector.tensor_tensor(
                out=code_rows[tile // 2][:, tile % 2, K1 + K_PASS * g0 : K1 + K_PASS * g1],
                in0=old_bytes[tile // 2][:, tile % 2, k].bitcast(FP8),
                in1=scale_all[:, k],
                op=MULT,
            )

        def permute(tile):
            pm = work.tile([P, PASSES, 2, P], F32, name=f"permuted_{tile}", tag="permuted", bufs=3)
            words = code_rows[tile // 2][:, tile % 2, :].bitcast(F32)
            nc.scalar.copy(out=pm[:], in_=words.rearrange("p (g w u) -> p g u w", g=PASSES, u=2))
            permuted[tile] = pm

        def code_transposes(tile):
            gr = work.tile([P, PASSES, P, PACK], BF16, name=f"grouped_{tile}", tag="grouped", bufs=3, align_bytes=64)
            grouped[tile] = gr
            for g0 in (0, 2):
                bank = psum.tile([P, 2, 2, P], F32, name=f"code_bank_{tile}_{g0}", tag="code_bank", bufs=2)
                for s in range(2):
                    g = g0 + s
                    for u in range(2):
                        if tile in permuted:
                            words = permuted[tile][:, g, u, :]
                        else:
                            row = code_rows[tile // 2][:, tile % 2, K_PASS * g : K_PASS * (g + 1)]
                            words = row.bitcast(F32)[:, u : K_PASS // 2 : 2]
                        nc.tensor.transpose(bank[:, s, u, :], words, ident[:])
                nc.scalar.copy(out=gr[:, g0 : g0 + 2, :, :].bitcast(F32), in_=bank[:].rearrange("p s u m -> p s m u"))

        def code_quantize(tile, g0=0, g1=PASSES):
            if g0 == 0:
                codes = work.tile([P, PASSES, P], U32, name=f"code_codes_{tile}", tag="code_codes", bufs=3, align_bytes=64)
                scales = work.tile([P, PASSES, P], U8, name=f"code_scales_{tile}", tag="code_scales", bufs=3, align_bytes=64)
                code_ops[tile] = (codes, scales)
            codes, scales = code_ops[tile]
            nc.vector.quantize_mx(
                out=codes[:, g0:g1, :].rearrange("p g m -> p (g m)").bitcast(FP8X4),
                scales=scales[:, g0:g1, :].rearrange("p g m -> p (g m)"),
                in_=grouped[tile][:, g0:g1, :, :].rearrange("p g m t -> p (g m t)"),
            )

        def stage1(tile, h):
            acc = psum.tile([P, NH], F32, name=f"stage1_{tile}_{h}", tag="acc", bufs=5)
            codes, scales = code_ops[tile]
            order = [1, 0, 2, 3] if h == 0 else [1, 2, 3, 0]
            for n, g in enumerate(order):
                if g == 0:
                    rhs = data_codes[h][:].bitcast(FP8X4)
                    rhs_scale = data_scales[h][:]
                else:
                    rhs = old_code[h][:, g - 1, :].bitcast(FP4X4)
                    rhs_scale = old_plane[:, g - 1, NH * h : NH * (h + 1)]
                nc.tensor.matmul_mx(
                    out=acc[:],
                    lhsT=codes[:, g, :].bitcast(FP8X4),
                    lhsT_scale=scales[:, g, :],
                    rhs=rhs,
                    rhs_scale=rhs_scale,
                    start=(n == 0),
                    stop=(n == PASSES - 1),
                )
            sums[tile, h] = acc

        def evacuate(tile, h):
            copy = work.tile([P, NH], F32, name=f"sum_{tile}_{h}", tag="sum", bufs=1)
            nc.scalar.copy(out=copy[:], in_=sums[tile, h][:])
            sums[tile, h] = copy

        def add_mask(tile, h):
            if h == 0:
                mt = work.tile([P, F], F32, name=f"masked_{tile}", tag="masked", bufs=2)
                masked[tile] = mt
            cols = slice(NH * h, NH * (h + 1))
            nc.vector.tensor_tensor(
                out=masked[tile][:, cols], in0=sums[tile, h][:], in1=mask_tiles[tile // 2][:, tile % 2, cols], op=ADD
            )

        def scale_features(tile):
            c = work.tile([P, 2, F // PACK, 2], BF16, name=f"coded_{tile}", tag="coded", bufs=2, align_bytes=64)
            nc.vector.tensor_tensor(
                out=c[:],
                in0=masked[tile][:].rearrange("p (w u e) -> p u w e", u=2, e=2),
                in1=feature_all[:].rearrange("p (w u e) -> p u w e", u=2, e=2),
                op=MULT,
            )
            coded[tile] = c

        def coded_transposes(copy, tile):
            bank = psum.tile([P, X_PASSES, 2, P], F32, name=f"coded_bank_{tile}", tag="coded_bank", bufs=1)
            words = coded[tile][:].rearrange("p u w e -> p (u w e)").bitcast(F32)
            for g in range(X_PASSES):
                for u in range(2):
                    first = (X_PASSES * u + g) * P
                    nc.tensor.transpose(bank[:, g, u, :], words[:, first : first + P], ident[:])
            cg = work.tile([P, X_PASSES, P, PACK], BF16, name=f"coded_grouped_{tile}", tag="coded_grouped", bufs=2, align_bytes=64)
            copy(out=cg[:].bitcast(F32), in_=bank[:].rearrange("p g u m -> p g m u"))
            coded_grouped[tile] = cg

        def coded_quantize(tile):
            codes = work.tile([P, X_PASSES, P], U32, name=f"coded_codes_{tile}", tag="coded_codes", bufs=2, align_bytes=64)
            scales = work.tile([P, X_PASSES, P], U8, name=f"coded_scales_{tile}", tag="coded_scales", bufs=2, align_bytes=64)
            nc.vector.quantize_mx(
                out=codes[:].rearrange("p g m -> p (g m)").bitcast(FP8X4),
                scales=scales[:].rearrange("p g m -> p (g m)"),
                in_=coded_grouped[tile][:].rearrange("p g m t -> p (g m t)"),
            )
            coded_ops[tile] = (codes, scales)

        def stage2(tile, on_vector=()):
            codes, scales = coded_ops[tile]
            result = work.tile([P, B], F32, name=f"result_{tile}", tag="result", bufs=3)
            blocks = 1 if tile == TILES - 1 else 2
            for b in range(X_BLOCKS):
                cols = slice(NH * b, NH * (b + 1))
                acc = psum.tile([P, NH], F32, name=f"stage2_{tile}_{b}", tag="acc", bufs=5)
                for g in range(X_PASSES):
                    nc.tensor.matmul_mx(
                        out=acc[:],
                        lhsT=codes[:, g, :].bitcast(FP8X4),
                        lhsT_scale=scales[:, g, :],
                        rhs=x_code[g][:, FP4_BYTES * NH * b : FP4_BYTES * NH * (b + 1)].bitcast(FP4X4),
                        rhs_scale=x_plane[:, g, cols],
                        start=(g == 0),
                        stop=(g == X_PASSES - 1),
                    )
                copy = vector_copy if b in on_vector else scalar_copy
                copy(out=result[:, cols], in_=acc[:])
                if (b + 1) % blocks == 0:
                    stored = slice(NH * (b + 1 - blocks), NH * (b + 1))
                    nc.sync.dma_start(out=out_rows[tile // 2, tile % 2, :, stored], in_=result[:, stored])

        def warm_up(count):
            bank = psum.tile([P, NH], F32, name="warm_up", tag="acc", bufs=5)
            rows = code_rows[0][:, 0, 0:NH]
            for n in range(count):
                nc.tensor.matmul(bank[:], lhsT=rows[:, 0:P], rhs=rows, start=True, stop=True)

        for g in range(OLD_PASSES):
            product(0, g, g + 1)
        code_transposes(0)
        data_interleave(scalar_copy, 0, 0, NH // 2)
        data_interleave(vector_copy, 0, NH // 2, NH)
        spread_features(0)
        spread_features(1)
        product(1)
        warm_up(6)
        data_interleave(scalar_copy, 1, 0, NH)
        code_transposes(1)
        product(3)
        code_quantize(0, 0, 2)
        code_quantize(0, 2, 4)
        data_quantize(0)
        permute(3)
        product(2)
        data_quantize(1)
        stage1(0, 0)
        stage1(0, 1)
        add_mask(0, 0)
        code_quantize(1)
        code_transposes(2)
        stage1(1, 0)
        stage1(1, 1)
        add_mask(0, 1)
        scale_features(0)
        code_quantize(2)
        coded_transposes(scalar_copy, 0)
        code_transposes(3)
        add_mask(1, 0)
        add_mask(1, 1)
        stage1(2, 1)
        product(4)
        coded_quantize(0)
        stage1(2, 0)
        scale_features(1)
        code_quantize(3)
        evacuate(2, 1)
        add_mask(2, 0)
        permute(4)
        add_mask(2, 1)
        stage2(0, on_vector=(3,))
        coded_transposes(scalar_copy, 1)
        scale_features(2)
        coded_quantize(1)

        for i in range(3, TILES - 1):
            stage1(i, 0)
            add_mask(i, 0)
            code_transposes(i + 1)
            if i + 2 < TILES:
                product(i + 2)
            coded_transposes(scalar_copy, i - 1)
            stage1(i, 1)
            code_quantize(i + 1)
            add_mask(i, 1)
            if i + 2 < TILES:
                permute(i + 2)
            stage2(i - 2)
            coded_quantize(i - 1)
            scale_features(i)

        last = TILES - 1
        stage1(last, 0)
        stage1(last, 1)
        coded_transposes(scalar_copy, last - 1)
        add_mask(last, 0)
        add_mask(last, 1)
        scale_features(last)
        stage2(last - 2)
        coded_quantize(last - 1)
        coded_transposes(vector_copy, last)
        coded_quantize(last)
        stage2(last - 1, on_vector=(2,))
        stage2(last, on_vector=(2,))
